import numpy as np
import ml_dtypes


def mxq(x, axis, fmt="e4m3"):
    dtype, down = {"e4m3": (ml_dtypes.float8_e4m3fn, 7), "e5m2": (ml_dtypes.float8_e5m2, 14)}[fmt]
    v = np.moveaxis(np.asarray(x, np.float32).astype(ml_dtypes.bfloat16).astype(np.float64), axis, -1)
    blocks = v.reshape(v.shape[:-1] + (-1, 32))
    amax = np.abs(blocks).max(-1, keepdims=True)
    byte = np.maximum(np.where(amax > 0, np.frexp(amax)[1] - 1 + 127, 0) - down, 1)
    scale = np.exp2(byte - 127.0)
    codes = (blocks / scale).astype(np.float32).astype(dtype).astype(np.float64)
    return np.moveaxis((codes * scale).reshape(v.shape), -1, axis)


WIDE = False


def mx_kscale(k):
    if not WIDE:
        return np.ones(k)
    levels = np.array([10, -10, 5, -5, 0])
    if k % 512:
        return np.exp2(np.random.permutation(np.resize(levels, k // 32))).repeat(32)
    a = np.empty((k // 512, 16))
    for p in range(k // 512):
        a[p, :8] = np.random.permutation(np.resize(levels, 8))
        for g in range(8):
            far = levels[np.abs(levels - a[p, g]) >= 10]
            a[p, g + 8] = far[np.random.randint(len(far))]
    return np.exp2(a.ravel()).repeat(32)


BF16 = ml_dtypes.bfloat16


def bf(x):
    return np.asarray(x, np.float32).astype(BF16)


def f64(x):
    return np.asarray(x).astype(np.float64)


E2M1 = np.array([0.0, 0.5, 1.0, 1.5, 2.0, 3.0, 4.0, 6.0, -0.0, -0.5, -1.0, -1.5, -2.0, -3.0, -4.0, -6.0])


def pack_weight(w, fmt):
    k, n = w.shape
    w = f64(bf(w)).reshape(k // 32, 32, n)
    amax = np.abs(w).max(1)
    if fmt == "e4m3":
        byte = np.frexp(amax)[1] - 1 + 127 - 7
    else:
        mant, ex = np.frexp(amax / 6.0)
        byte = np.where(mant > 0.5, ex, ex - 1) + 127
    byte = np.clip(np.where(amax > 0, byte, 1), 1, 254)
    scaled = (w * np.exp2(127.0 - byte)[:, None, :]).reshape(k, n).astype(np.float32)
    by_word = np.ascontiguousarray(scaled.reshape(k // 512, 128, 4, n).transpose(0, 1, 3, 2))
    if fmt == "e4m3":
        words = by_word.astype(ml_dtypes.float8_e4m3fn).view(np.uint8)
    else:
        c = by_word.astype(ml_dtypes.float4_e2m1fn).view(np.uint8) & 0xF
        words = c[..., 0::2] | (c[..., 1::2] << 4)
    return np.ascontiguousarray(words), np.ascontiguousarray(byte.astype(np.uint8).reshape(k // 512, 16, n))


def unpack_weight(words, scales, fmt):
    g, p, n, _ = words.shape
    if fmt == "e4m3":
        vals = np.ascontiguousarray(words).view(ml_dtypes.float8_e4m3fn).astype(np.float64)
    else:
        nib = np.empty((g, p, n, 4), np.uint8)
        nib[..., 0::2] = words & 0xF
        nib[..., 1::2] = words >> 4
        vals = E2M1[nib]
    vals = vals * np.repeat(np.exp2(scales.astype(np.float64) - 127.0), 8, axis=1)[..., None]
    return vals.transpose(0, 1, 3, 2).reshape(g * 512, n)
def pack4(w):
    words, scales = pack_weight(w, "e2m1")
    return words.reshape(words.shape[0], 128, -1), scales


def unpack4(words, scales):
    return unpack_weight(words.reshape(words.shape[0], 128, -1, 2), scales, "e2m1")


def planes(Y):
    n, m = Y.shape
    b = f64(bf(Y)).reshape(n // 32, 32, m)
    amax = np.abs(b).max(1)
    byte = np.clip(np.where(amax > 0, np.frexp(amax)[1] - 1 + 127 - 7, 1), 1, 254)
    codes = (b * np.exp2(127.0 - byte)[:, None, :]).reshape(n, m).astype(np.float32).astype(ml_dtypes.float8_e4m3fn).view(np.uint8)
    words = codes.reshape(n // 512, 128, 4, m).transpose(0, 1, 3, 2)
    return np.ascontiguousarray(words), np.ascontiguousarray(byte.astype(np.uint8).reshape(n // 512, 16, m))


T, D, R, N = 1024, 1024, 1024, 1024


def softplus(v):
    return np.maximum(v, 0.0) + np.log1p(np.exp(-np.abs(v)))


def sigmoid(v):
    return 1.0 / (1.0 + np.exp(-v))


def setup_inputs():
    s, u, t = mx_kscale(D), mx_kscale(R), mx_kscale(T)
    x = bf(np.random.standard_normal((T, D)) * s)
    w_words, w_scales = pack4(np.random.standard_normal((D, N)) / np.sqrt(D) / s[:, None])
    r = bf(np.random.standard_normal((T, R)) * u)
    l_words, l_scales = pack4(0.7 * np.random.standard_normal((R, N)) / np.sqrt(R) / u[:, None])
    return {"x": x,
            "w_words": w_words,
            "w_scales": w_scales,
            "r": r,
            "l_words": l_words,
            "l_scales": l_scales,
            "trace": bf(np.random.standard_normal((T, D)) * t[:, None]),
            "g": bf((1.0 + 0.1 * np.random.standard_normal(T)) / t)}


def core(x, w_words, w_scales, r, l_words, l_scales, trace, g):
    steps = x.shape[0]
    y = (mxq(f64(x), 1, "e4m3") @ unpack4(w_words, w_scales)) - (mxq(f64(r), 1, "e4m3") @ unpack4(l_words, l_scales))
    a = softplus(y)
    theta = np.mean(a * a, axis=0)
    phi = a * (a - theta[None, :]) * sigmoid(y)
    pm = f64(g)[:, None] * phi
    return (mxq(f64(trace), 0, "e4m3").T @ mxq(pm, 0, "e4m3")) / np.sqrt(steps)


def reference(x, w_words, w_scales, r, l_words, l_scales, trace, g):
    R_out = core(x, w_words, w_scales, r, l_words, l_scales, trace, g)
    words, scales = planes(R_out)
    return R_out, words, scales

@@ -1,0 +1,401 @@
+from contextlib import ExitStack
+
+import concourse.mybir as mybir
+from concourse.masks import make_identity
+
+T, D, R, N = 1024, 1024, 1024, 1024
+FLOPS = 2 * T * D * N + 2 * T * R * N + 2 * D * T * N
+
+F32 = mybir.dt.float32
+BF16 = mybir.dt.bfloat16
+U32 = mybir.dt.uint32
+I32 = mybir.dt.int32
+U8 = mybir.dt.uint8
+FP8X4 = mybir.dt.float8_e4m3fn_x4
+FP4X4 = mybir.dt.float4_e2m1fn_x4
+ALU = mybir.AluOpType
+ACT = mybir.ActivationFunctionType
+
+P = 128
+PACK = 4
+K_PASS = P * PACK
+GROUPS = 2
+N_TILES = N // P
+BANK = 512
+LINEAR_FROM = 20.0
+WARM = 0
+INV_SQRT_T = 1.0 / 32.0
+
+
+def tile_bcmslidingthresholdtraceupdate_x2_kernel(
+    tc, x, w_words, w_scales, r, l_words, l_scales, trace, g, out_0, out_1, out_2
+):
+    nc = tc.nc
+    with ExitStack() as ctx:
+        keep = ctx.enter_context(tc.tile_pool(name="keep", bufs=1))
+        work = ctx.enter_context(tc.tile_pool(name="work", bufs=1))
+        psum = ctx.enter_context(tc.psum_pool(name="psum", bufs=4))
+        ctx.enter_context(tc.manual_schedule())
+
+        warm_in = keep.tile([P, 1], F32, name="warm_in")
+        warm_out = keep.tile([P, 1], F32, name="warm_out")
+        nc.vector.memset(warm_in[:], 0.0)
+        nc.scalar.activation(out=warm_out[:], in_=warm_in[:], func=ACT.Sigmoid)
+
+        zeros = keep.tile([P, BANK], BF16, name="zeros")
+        nc.vector.memset(zeros[:], 0.0)
+
+        def keep_clock(bank_ap):
+            nc.tensor.matmul(bank_ap, lhsT=zeros[:, 0:P], rhs=zeros[:], start=True, stop=True)
+
+        for i in range(WARM):
+            wbank = psum.tile([P, BANK], F32, name="wbank", tag="z")
+            keep_clock(wbank[:])
+
+        ident = keep.tile([P, P], F32, name="ident")
+        make_identity(nc, ident[:])
+
+        wscale = {}
+        for name in ("w", "l"):
+            wscale[name] = keep.tile([P, GROUPS, N], U8, name=name + "_scale", align_bytes=64)
+            nc.vector.memset(wscale[name][:].rearrange("p g n -> p (g n)").bitcast(I32), 0)
+
+        act_src = {"x": x, "r": r}
+        raw = {}
+
+        def load_act(name, tg, jp):
+            t_ = keep.tile([P, 2, D], BF16, name="raw_%s%d%d" % (name, tg, jp), align_bytes=64)
+            rows = act_src[name][tg * K_PASS:(tg + 1) * K_PASS, :].rearrange("(p j) k -> p j k", j=PACK)
+            nc.sync.dma_start(out=t_[:], in_=rows[:, 2 * jp:2 * jp + 2, :])
+            raw[name, tg, jp] = t_
+
+        w_src = {"w": w_words, "l": l_words}
+        s_src = {"w": w_scales, "l": l_scales}
+        wcode = {}
+
+        def load_words(name, half):
+            t_ = keep.tile([P, GROUPS, N], U8, name="words_%s%d" % (name, half), align_bytes=64)
+            src = w_src[name][:, :, half * N:(half + 1) * N].rearrange("g p b -> p g b")
+            nc.sync.dma_start(out=t_[:].bitcast(I32), in_=src.bitcast(I32))
+            wcode[name, half] = t_
+
+        def load_scales(name):
+            for q in range(4):
+                src = s_src[name][:, 4 * q:4 * q + 4, :].rearrange("g r n -> r g n")
+                nc.sync.dma_start(out=wscale[name][32 * q:32 * q + 4, :, :].bitcast(I32), in_=src.bitcast(I32))
+
+        traw = {}
+
+        def load_trace(tg):
+            t_ = keep.tile([P, PACK, D], BF16, name="traw%d" % tg, align_bytes=64)
+            nc.sync.dma_start(out=t_[:], in_=trace[tg * K_PASS:(tg + 1) * K_PASS, :].rearrange("(p j) d -> p j d", j=PACK))
+            traw[tg] = t_
+
+        load_act("r", 0, 0)
+        load_act("r", 0, 1)
+        load_scales("l")
+        load_words("l", 0)
+        load_act("x", 0, 0)
+        load_act("x", 0, 1)
+        load_scales("w")
+        load_words("w", 0)
+        load_trace(0)
+        load_act("r", 1, 0)
+        load_act("r", 1, 1)
+        load_act("x", 1, 0)
+        load_act("x", 1, 1)
+        load_trace(1)
+        load_words("l", 1)
+        load_words("w", 1)
+        g_raw = keep.tile([P, GROUPS, PACK], BF16, name="g_raw")
+        nc.sync.dma_start(out=g_raw[:], in_=g.rearrange("(g p j) -> p g j", g=GROUPS, j=PACK))
+
+        grouped = {}
+        acode = {}
+        ascale = {}
+
+        def turn(name, tg, jp, kp, warm):
+            words = raw[name, tg, jp][:].rearrange("p j k -> p (j k)").bitcast(F32)
+            bank = psum.tile([P, 2, 2, P], F32, name="tbank", tag="t")
+            if warm:
+                keep_clock(bank[:].rearrange("p u j t -> p (u j t)"))
+            for jj in range(2):
+                for u in range(2):
+                    base = jj * (D // 2) + kp * 256
+                    nc.tensor.transpose(bank[:, u, jj, :], words[:, base + u:base + 256:2], ident[:])
+            grouped[name, tg, jp, kp] = work.tile([P, 2 * BANK], BF16, name="grouped", tag="grouped", bufs=6, align_bytes=64)
+            dst = grouped[name, tg, jp, kp][:]
+            if name == "r":
+                nc.scalar.copy(out=dst.bitcast(F32).rearrange("p (c u) -> p c u", u=2),
+                               in_=bank[:].rearrange("p u j t -> p (j t) u"))
+            else:
+                src = bank[:].rearrange("p u j t -> p (u j t)").bitcast(BF16).rearrange("p (u c e) -> p c u e", u=2, e=2)
+                nc.vector.tensor_scalar(out=dst.rearrange("p (c u e) -> p c u e", u=2, e=2), in0=src,
+                                        scalar1=-1.0, scalar2=None, op0=ALU.mult)
+
+        def quant_act(name, tg, jp, kp):
+            if jp == 0:
+                acode[name, tg, kp] = keep.tile([P, BANK], U32, name="acode_%s%d%d" % (name, tg, kp), align_bytes=64)
+                ascale[name, tg, kp] = keep.tile([P, BANK], U8, name="ascale_%s%d%d" % (name, tg, kp), align_bytes=64)
+            cols = slice(jp * 2 * P, (jp + 1) * 2 * P)
+            nc.vector.quantize_mx(out=acode[name, tg, kp][:, cols].bitcast(FP8X4), scales=ascale[name, tg, kp][:, cols],
+                                  in_=grouped[name, tg, jp, kp][:])
+
+        tcode = {}
+        tscale = {}
+        tgrouped = {}
+
+        def trace_interleave(tg, dg):
+            t_ = work.tile([P, 4 * BANK], BF16, name="tgrouped", tag="tgrouped", bufs=2, align_bytes=64)
+            nc.vector.tensor_copy(
+                out=t_[:].rearrange("p (s m j) -> p s m j", s=PACK, j=PACK),
+                in_=traw[tg][:, :, dg * K_PASS:(dg + 1) * K_PASS].rearrange("p j (m s) -> p s m j", s=PACK))
+            tgrouped[tg, dg] = t_
+
+        def trace_quant(tg, dg):
+            tcode[tg, dg] = keep.tile([P, BANK], U32, name="tcode%d%d" % (tg, dg), align_bytes=64)
+            tscale[tg, dg] = keep.tile([P, BANK], U8, name="tscale%d%d" % (tg, dg), align_bytes=64)
+            nc.vector.quantize_mx(out=tcode[tg, dg][:].bitcast(FP8X4), scales=tscale[tg, dg][:], in_=tgrouped[tg, dg][:])
+
+        zbank = {}
+        sn = {}
+        ln = {}
+        na = {}
+        u_ = {}
+        wv = {}
+        part = keep.tile([P, N_TILES, GROUPS], F32, name="part")
+        theta = keep.tile([P, N_TILES], F32, name="theta")
+        neg_g = keep.tile([P, GROUPS, PACK], F32, name="neg_g")
+
+        passes = [("r", "l", 0), ("r", "l", 1), ("x", "w", 0), ("x", "w", 1)]
+
+        def drive(n, tg, i0=0, i1=4):
+            if i0 == 0:
+                zbank[n, tg] = psum.tile([P, BANK], F32, name="zbank", tag="z")
+            half, col = divmod(n, 4)
+            for i in range(i0, i1):
+                a_name, w_name, kp = passes[i]
+                nc.tensor.matmul_mx(
+                    out=zbank[n, tg][:],
+                    lhsT=wcode[w_name, half][:, kp, col * 2 * P:(col + 1) * 2 * P].bitcast(FP4X4),
+                    lhsT_scale=wscale[w_name][:, kp, n * P:(n + 1) * P],
+                    rhs=acode[a_name, tg, kp][:].bitcast(FP8X4),
+                    rhs_scale=ascale[a_name, tg, kp][:],
+                    start=(i == 0), stop=(i == len(passes) - 1))
+
+        def sigmoid(n, tg):
+            sn[n, tg] = work.tile([P, BANK], F32, name="sn", tag="sn", bufs=8)
+            nc.scalar.activation(out=sn[n, tg][:], in_=zbank[n, tg][:], func=ACT.Sigmoid)
+
+        def log(n, tg):
+            ln[n, tg] = work.tile([P, BANK], F32, name="ln", tag="ln", bufs=4)
+            nc.scalar.activation(out=ln[n, tg][:], in_=sn[n, tg][:], func=ACT.Ln)
+
+        def rate(n, tg):
+            na[n, tg] = work.tile([P, BANK], F32, name="na", tag="na", bufs=12)
+            nc.vector.scalar_tensor_tensor(out=na[n, tg][:], in0=ln[n, tg][:], scalar=-LINEAR_FROM, in1=zbank[n, tg][:],
+                                           op0=ALU.max, op1=ALU.min)
+
+        def square(n, tg):
+            junk = work.tile([P, BANK], BF16, name="junk", tag="junk", bufs=2)
+            nc.scalar.activation(out=junk[:], in_=na[n, tg][:], func=ACT.Square, scale=INV_SQRT_T,
+                                 accum_out=part[:, n, tg:tg + 1])
+
+        def slope(n, tg):
+            u_[n, tg] = work.tile([P, BANK], F32, name="u", tag="u", bufs=12)
+            nc.vector.scalar_tensor_tensor(out=u_[n, tg][:], in0=sn[n, tg][:], scalar=1.0, in1=na[n, tg][:],
+                                           op0=ALU.subtract, op1=ALU.mult)
+
+        def threshold(n0, n1):
+            nc.vector.tensor_tensor(out=theta[:, n0:n1], in0=part[:, n0:n1, 0], in1=part[:, n0:n1, 1], op=ALU.add)
+
+        def bcm(n, tg):
+            wv[n, tg] = work.tile([P, BANK], F32, name="wv", tag="wv", bufs=4)
+            nc.vector.scalar_tensor_tensor(out=wv[n, tg][:], in0=na[n, tg][:], scalar=theta[:, n:n + 1], in1=u_[n, tg][:],
+                                           op0=ALU.add, op1=ALU.mult)
+
+        pbank = {}
+        pm = {}
+        pcode = {}
+        pscale = {}
+
+        def turn_back(n, tg):
+            bank = psum.tile([P, PACK, P], F32, name="pbank", tag="t")
+            for j in range(PACK):
+                nc.tensor.transpose(bank[:, j, :], wv[n, tg][:, j * P:(j + 1) * P], ident[:])
+            pbank[n, tg] = bank
+
+        def gain(n, tg):
+            if tg == 0:
+                pm[n] = work.tile([P, GROUPS, P, PACK], BF16, name="pm", tag="pm", bufs=2, align_bytes=64)
+            nc.vector.tensor_tensor(out=pm[n][:, tg, :, :], in0=pbank[n, tg][:].rearrange("p j n -> p n j"),
+                                    in1=neg_g[:, tg, :].unsqueeze(1).to_broadcast([P, P, PACK]), op=ALU.mult)
+
+        def quant_pm(n):
+            pcode[n] = work.tile([P, GROUPS * P], U32, name="pcode", tag="pcode", bufs=2, align_bytes=64)
+            pscale[n] = work.tile([P, GROUPS * P], U8, name="pscale", tag="pscale", bufs=2, align_bytes=64)
+            nc.vector.quantize_mx(out=pcode[n][:].bitcast(FP8X4), scales=pscale[n][:],
+                                  in_=pm[n][:].rearrange("p g n j -> p (g n j)"))
+
+        obank = {}
+        of32 = {}
+        obf = {}
+        ocode = keep.tile([P, GROUPS, N], U32, name="ocode", align_bytes=64)
+        oscale = keep.tile([P, GROUPS, N], U8, name="oscale", align_bytes=64)
+
+        def correlate(n, dg):
+            bank = psum.tile([P, PACK, P], F32, name="obank", tag="t")
+            for s in range(PACK):
+                for tg in range(GROUPS):
+                    nc.tensor.matmul_mx(
+                        out=bank[:, s, :],
+                        lhsT=tcode[tg, dg][:, s * P:(s + 1) * P].bitcast(FP8X4),
+                        lhsT_scale=tscale[tg, dg][:, s * P:(s + 1) * P],
+                        rhs=pcode[n][:, tg * P:(tg + 1) * P].bitcast(FP8X4),
+                        rhs_scale=pscale[n][:, tg * P:(tg + 1) * P],
+                        start=(tg == 0), stop=(tg == GROUPS - 1))
+            obank[n, dg] = bank
+
+        def out_copy(n, dg):
+            if n % 2 == 0:
+                of32[n // 2, dg] = work.tile([P, PACK, 2 * P], F32, name="of32", tag="of32", bufs=4)
+            c0 = (n % 2) * P
+            nc.scalar.activation(out=of32[n // 2, dg][:, :, c0:c0 + P], in_=obank[n, dg][:], func=ACT.Copy, scale=INV_SQRT_T)
+
+        def out_cast(n, dg):
+            obf[n, dg] = work.tile([P, P, PACK], BF16, name="obf", tag="obf", bufs=4, align_bytes=64)
+            c0 = (n % 2) * P
+            nc.vector.tensor_copy(out=obf[n, dg][:], in_=of32[n // 2, dg][:, :, c0:c0 + P].rearrange("p s n -> p n s"))
+
+        def out_quant(n, dg):
+            nc.vector.quantize_mx(out=ocode[:, dg, n * P:(n + 1) * P].bitcast(FP8X4), scales=oscale[:, dg, n * P:(n + 1) * P],
+                                  in_=obf[n, dg][:].rearrange("p n s -> p (n s)"))
+
+        def out_cast_psum(n, dg):
+            obf[n, dg] = work.tile([P, P, PACK], BF16, name="obf", tag="obf", bufs=4, align_bytes=64)
+            nc.scalar.activation(out=obf[n, dg][:], in_=obank[n, dg][:].rearrange("p s n -> p n s"), func=ACT.Copy, scale=INV_SQRT_T)
+
+        def out_cast_s(n, dg):
+            obf[n, dg] = work.tile([P, P, PACK], BF16, name="obf", tag="obf", bufs=4, align_bytes=64)
+            c0 = (n % 2) * P
+            nc.scalar.copy(out=obf[n, dg][:], in_=of32[n // 2, dg][:, :, c0:c0 + P].rearrange("p s n -> p n s"))
+
+        def store_f32(n0, n1, dg):
+            rows = out_0[dg * K_PASS:(dg + 1) * K_PASS, n0 * P:n1 * P].rearrange("(p s) n -> p s n", s=PACK)
+            c0 = (n0 % 2) * P
+            nc.sync.dma_start(out=rows, in_=of32[n0 // 2, dg][:, :, c0:c0 + (n1 - n0) * P])
+
+        def store_words(n0, n1):
+            dst = out_1.rearrange("g p m t -> p g (m t)")[:, :, n0 * P * PACK:n1 * P * PACK]
+            nc.sync.dma_start(out=dst.bitcast(I32), in_=ocode[:, :, n0 * P:n1 * P].bitcast(I32))
+
+        def store_scales():
+            for q in range(4):
+                dst = out_2[:, 4 * q:4 * q + 4, :].rearrange("g r n -> r g n")
+                nc.scalar.dma_start(out=dst.bitcast(I32), in_=oscale[32 * q:32 * q + 4, :, :].bitcast(I32))
+
+        batches = [[(n, tg) for n in (2 * k, 2 * k + 1) for tg in range(GROUPS)] for k in range(4)]
+
+        def each(fn, k, lo=0, hi=4):
+            for b in batches[k][lo:hi]:
+                fn(*b)
+
+        def both(fn, n):
+            fn(n, 0)
+            fn(n, 1)
+
+        def logs_and_rates(k):
+            for b in batches[k]:
+                log(*b)
+                rate(*b)
+
+        def turns(name, tg, jp, warm=True):
+            turn(name, tg, jp, 0, warm)
+            turn(name, tg, jp, 1, warm)
+
+        def quants(name, tg, jp):
+            quant_act(name, tg, jp, 0)
+            quant_act(name, tg, jp, 1)
+
+        def to_time(n):
+            both(bcm, n)
+            both(turn_back, n)
+
+        def stage2(n):
+            quant_pm(n)
+            both(correlate, n)
+
+        def stores(n0, n1):
+            store_f32(n0, n1, 0)
+            store_f32(n0, n1, 1)
+
+        for tg in range(GROUPS):
+            turns("r", tg, 0, False and tg == 0)
+            turns("r", tg, 1, False)
+            quants("r", tg, 0)
+            if tg == 1:
+                both(trace_quant, 0)
+            turns("x", tg, 0, False)
+            quants("r", tg, 1)
+            turns("x", tg, 1, False)
+            quants("x", tg, 0)
+            for n in (0, 1):
+                drive(n, tg, 0, 2)
+            quants("x", tg, 1)
+            for n in (0, 1):
+                drive(n, tg, 2, 4)
+                sigmoid(n, tg)
+            both(trace_interleave, tg)
+        nc.vector.tensor_scalar(out=neg_g[:], in0=g_raw[:], scalar1=-1.0, scalar2=None, op0=ALU.mult)
+        for k in range(4):
+            a, b = 2 * k, 2 * k + 1
+            last = k == 3
+            logs_and_rates(k)
+            if not last:
+                each(drive, k + 1)
+            if k > 0 and not last:
+                both(out_copy, a - 2)
+                both(out_copy, b - 2)
+                stores(a - 2, a)
+            each(square, k)
+            if last:
+                both(out_copy, a - 2)
+                both(out_copy, b - 2)
+                stores(a - 2, a)
+                both(out_cast_s, a - 2)
+                both(out_cast_s, b - 2)
+            else:
+                each(sigmoid, k + 1)
+            each(slope, k)
+            if k == 0:
+                both(trace_quant, 1)
+            elif not last:
+                both(out_cast, a - 2)
+                both(out_cast, b - 2)
+            threshold(a, b + 1)
+            if 0 < k < 3:
+                both(out_quant, a - 2)
+                both(out_quant, b - 2)
+                store_words(a - 2, a)
+            to_time(a)
+            to_time(b)
+            both(gain, a)
+            gain(b, 0)
+            stage2(a)
+            gain(b, 1)
+            if last:
+                both(out_quant, a - 2)
+                both(out_quant, b - 2)
+                store_words(a - 2, a)
+            stage2(b)
+        both(out_copy, 6)
+        stores(6, 7)
+        both(out_cast, 6)
+        both(out_copy, 7)
+        stores(7, 8)
+        both(out_quant, 6)
+        store_words(6, 7)
+        both(out_cast, 7)
+        both(out_quant, 7)
+        store_words(7, 8)
+        store_scales()

@@ -23,7 +23,6 @@ GROUPS = 2
 N_TILES = N // P
 BANK = 512
 LINEAR_FROM = 20.0
-WARM = 0
 INV_SQRT_T = 1.0 / 32.0
 
 
@@ -34,23 +33,13 @@ def tile_bcmslidingthresholdtraceupdate_x2_kernel(
     with ExitStack() as ctx:
         keep = ctx.enter_context(tc.tile_pool(name="keep", bufs=1))
         work = ctx.enter_context(tc.tile_pool(name="work", bufs=1))
-        psum = ctx.enter_context(tc.psum_pool(name="psum", bufs=4))
+        psum = ctx.enter_context(tc.psum_pool(name="psum", bufs=1))
         ctx.enter_context(tc.manual_schedule())
 
         warm_in = keep.tile([P, 1], F32, name="warm_in")
         warm_out = keep.tile([P, 1], F32, name="warm_out")
         nc.vector.memset(warm_in[:], 0.0)
         nc.scalar.activation(out=warm_out[:], in_=warm_in[:], func=ACT.Sigmoid)
-
-        zeros = keep.tile([P, BANK], BF16, name="zeros")
-        nc.vector.memset(zeros[:], 0.0)
-
-        def keep_clock(bank_ap):
-            nc.tensor.matmul(bank_ap, lhsT=zeros[:, 0:P], rhs=zeros[:], start=True, stop=True)
-
-        for i in range(WARM):
-            wbank = psum.tile([P, BANK], F32, name="wbank", tag="z")
-            keep_clock(wbank[:])
 
         ident = keep.tile([P, P], F32, name="ident")
         make_identity(nc, ident[:])
@@ -64,7 +53,7 @@ def tile_bcmslidingthresholdtraceupdate_x2_kernel(
         raw = {}
 
         def load_act(name, tg, jp):
-            t_ = keep.tile([P, 2, D], BF16, name="raw_%s%d%d" % (name, tg, jp), align_bytes=64)
+            t_ = work.tile([P, 2, D], BF16, name="raw", tag="raw", bufs=6, align_bytes=64)
             rows = act_src[name][tg * K_PASS:(tg + 1) * K_PASS, :].rearrange("(p j) k -> p j k", j=PACK)
             nc.sync.dma_start(out=t_[:], in_=rows[:, 2 * jp:2 * jp + 2, :])
             raw[name, tg, jp] = t_
@@ -100,34 +89,55 @@ def tile_bcmslidingthresholdtraceupdate_x2_kernel(
         load_scales("w")
         load_words("w", 0)
         load_trace(0)
-        load_act("r", 1, 0)
-        load_act("r", 1, 1)
         load_act("x", 1, 0)
         load_act("x", 1, 1)
-        load_trace(1)
-        load_words("l", 1)
-        load_words("w", 1)
         g_raw = keep.tile([P, GROUPS, PACK], BF16, name="g_raw")
-        nc.sync.dma_start(out=g_raw[:], in_=g.rearrange("(g p j) -> p g j", g=GROUPS, j=PACK))
+
+        def late_loads():
+            load_act("r", 1, 0)
+            load_act("r", 1, 1)
+            load_trace(1)
+            load_words("l", 1)
+            load_words("w", 1)
+            nc.sync.dma_start(out=g_raw[:], in_=g.rearrange("(g p j) -> p g j", g=GROUPS, j=PACK))
 
         grouped = {}
         acode = {}
         ascale = {}
 
-        def turn(name, tg, jp, kp, warm):
+        halves = {}
+
+        def sort_words(name, tg, jp):
+            halves[name, tg, jp] = work.tile([P, 4, 2, P], F32, name="halves", tag="halves", bufs=2)
+            rows = raw[name, tg, jp][:].rearrange("p j k -> p (j k)")
+            if name == "r":
+                nc.vector.tensor_copy(out=halves[name, tg, jp][:],
+                                      in_=rows.bitcast(F32).rearrange("p (c q u) -> p c u q", c=4, u=2))
+            else:
+                src = rows.rearrange("p (c q u e) -> p c u q e", c=4, u=2, e=2)
+                for u in range(2):
+                    dst = halves[name, tg, jp][:, :, u, :].bitcast(BF16).rearrange("p c (q e) -> p c q e", e=2)
+                    nc.vector.tensor_scalar(out=dst, in0=src[:, :, u, :, :], scalar1=-1.0, scalar2=None, op0=ALU.mult)
+
+        def turn(name, tg, jp, kp, how):
+            bank = psum.tile([P, 2, 2, P], F32, name="tbank", tag="bank%d" % (4 + 2 * jp + kp))
             words = raw[name, tg, jp][:].rearrange("p j k -> p (j k)").bitcast(F32)
-            bank = psum.tile([P, 2, 2, P], F32, name="tbank", tag="t")
-            if warm:
-                keep_clock(bank[:].rearrange("p u j t -> p (u j t)"))
             for jj in range(2):
                 for u in range(2):
-                    base = jj * (D // 2) + kp * 256
-                    nc.tensor.transpose(bank[:, u, jj, :], words[:, base + u:base + 256:2], ident[:])
-            grouped[name, tg, jp, kp] = work.tile([P, 2 * BANK], BF16, name="grouped", tag="grouped", bufs=6, align_bytes=64)
+                    if (name, tg, jp) in halves:
+                        src = halves[name, tg, jp][:, 2 * jj + kp, u, :]
+                    else:
+                        base = jj * (D // 2) + kp * 256
+                        src = words[:, base + u:base + 256:2]
+                    nc.tensor.transpose(bank[:, u, jj, :], src, ident[:])
+            grouped[name, tg, jp, kp] = work.tile([P, 2 * BANK], BF16, name="grouped", tag="grouped", bufs=8, align_bytes=64)
             dst = grouped[name, tg, jp, kp][:]
-            if name == "r":
+            if "s" in how:
                 nc.scalar.copy(out=dst.bitcast(F32).rearrange("p (c u) -> p c u", u=2),
                                in_=bank[:].rearrange("p u j t -> p (j t) u"))
+            elif "v" in how:
+                nc.vector.tensor_copy(out=dst.bitcast(F32).rearrange("p (c u) -> p c u", u=2),
+                                      in_=bank[:].rearrange("p u j t -> p (j t) u"))
             else:
                 src = bank[:].rearrange("p u j t -> p (u j t)").bitcast(BF16).rearrange("p (u c e) -> p c u e", u=2, e=2)
                 nc.vector.tensor_scalar(out=dst.rearrange("p (c u e) -> p c u e", u=2, e=2), in0=src,
@@ -161,18 +171,19 @@ def tile_bcmslidingthresholdtraceupdate_x2_kernel(
         sn = {}
         ln = {}
         na = {}
+        na_both = {}
         u_ = {}
         wv = {}
-        part = keep.tile([P, N_TILES, GROUPS], F32, name="part")
         theta = keep.tile([P, N_TILES], F32, name="theta")
         neg_g = keep.tile([P, GROUPS, PACK], F32, name="neg_g")
 
-        passes = [("r", "l", 0), ("r", "l", 1), ("x", "w", 0), ("x", "w", 1)]
+        pair_order = {0: (("r", "l"), ("x", "w")), 1: (("x", "w"), ("r", "l"))}
 
         def drive(n, tg, i0=0, i1=4):
             if i0 == 0:
-                zbank[n, tg] = psum.tile([P, BANK], F32, name="zbank", tag="z")
+                zbank[n, tg] = psum.tile([P, BANK], F32, name="zbank", tag="bank%d" % (n if n < 4 else 2 * (n % 2) + tg))
             half, col = divmod(n, 4)
+            passes = [(a_name, w_name, kp) for a_name, w_name in pair_order[tg] for kp in range(2)]
             for i in range(i0, i1):
                 a_name, w_name, kp = passes[i]
                 nc.tensor.matmul_mx(
@@ -192,27 +203,29 @@ def tile_bcmslidingthresholdtraceupdate_x2_kernel(
             nc.scalar.activation(out=ln[n, tg][:], in_=sn[n, tg][:], func=ACT.Ln)
 
         def rate(n, tg):
-            na[n, tg] = work.tile([P, BANK], F32, name="na", tag="na", bufs=12)
-            nc.vector.scalar_tensor_tensor(out=na[n, tg][:], in0=ln[n, tg][:], scalar=-LINEAR_FROM, in1=zbank[n, tg][:],
+            if tg == 0:
+                na_both[n] = work.tile([P, GROUPS, BANK], F32, name="na", tag="na", bufs=6)
+            na[n, tg] = na_both[n][:, tg, :]
+            nc.vector.scalar_tensor_tensor(out=na[n, tg], in0=ln[n, tg][:], scalar=-LINEAR_FROM, in1=zbank[n, tg][:],
                                            op0=ALU.max, op1=ALU.min)
 
-        def square(n, tg):
-            junk = work.tile([P, BANK], BF16, name="junk", tag="junk", bufs=2)
-            nc.scalar.activation(out=junk[:], in_=na[n, tg][:], func=ACT.Square, scale=INV_SQRT_T,
-                                 accum_out=part[:, n, tg:tg + 1])
+        def square(n):
+            junk = work.tile([P, T], BF16, name="junk", tag="junk", bufs=1)
+            nc.scalar.activation(out=junk[:], in_=na_both[n][:].rearrange("p g t -> p (g t)"), func=ACT.Square,
+                                 scale=INV_SQRT_T, accum_out=theta[:, n:n + 1])
 
         def slope(n, tg):
             u_[n, tg] = work.tile([P, BANK], F32, name="u", tag="u", bufs=12)
-            nc.vector.scalar_tensor_tensor(out=u_[n, tg][:], in0=sn[n, tg][:], scalar=1.0, in1=na[n, tg][:],
+            nc.vector.scalar_tensor_tensor(out=u_[n, tg][:], in0=sn[n, tg][:], scalar=1.0, in1=na[n, tg],
                                            op0=ALU.subtract, op1=ALU.mult)
-
-        def threshold(n0, n1):
-            nc.vector.tensor_tensor(out=theta[:, n0:n1], in0=part[:, n0:n1, 0], in1=part[:, n0:n1, 1], op=ALU.add)
 
         def bcm(n, tg):
             wv[n, tg] = work.tile([P, BANK], F32, name="wv", tag="wv", bufs=4)
-            nc.vector.scalar_tensor_tensor(out=wv[n, tg][:], in0=na[n, tg][:], scalar=theta[:, n:n + 1], in1=u_[n, tg][:],
+            nc.vector.scalar_tensor_tensor(out=wv[n, tg][:], in0=na[n, tg], scalar=theta[:, n:n + 1], in1=u_[n, tg][:],
                                            op0=ALU.add, op1=ALU.mult)
+
+        def pair_of(n):
+            return 2 * (n % 2) + (4 if n < 6 else 0)
 
         pbank = {}
         pm = {}
@@ -220,7 +233,7 @@ def tile_bcmslidingthresholdtraceupdate_x2_kernel(
         pscale = {}
 
         def turn_back(n, tg):
-            bank = psum.tile([P, PACK, P], F32, name="pbank", tag="t")
+            bank = psum.tile([P, PACK, P], F32, name="pbank", tag="bank%d" % (pair_of(n) + tg))
             for j in range(PACK):
                 nc.tensor.transpose(bank[:, j, :], wv[n, tg][:, j * P:(j + 1) * P], ident[:])
             pbank[n, tg] = bank
@@ -244,7 +257,7 @@ def tile_bcmslidingthresholdtraceupdate_x2_kernel(
         oscale = keep.tile([P, GROUPS, N], U8, name="oscale", align_bytes=64)
 
         def correlate(n, dg):
-            bank = psum.tile([P, PACK, P], F32, name="obank", tag="t")
+            bank = psum.tile([P, PACK, P], F32, name="obank", tag="bank%d" % (pair_of(n) + dg))
             for s in range(PACK):
                 for tg in range(GROUPS):
                     nc.tensor.matmul_mx(
@@ -294,7 +307,12 @@ def tile_bcmslidingthresholdtraceupdate_x2_kernel(
                 dst = out_2[:, 4 * q:4 * q + 4, :].rearrange("g r n -> r g n")
                 nc.scalar.dma_start(out=dst.bitcast(I32), in_=oscale[32 * q:32 * q + 4, :, :].bitcast(I32))
 
-        batches = [[(n, tg) for n in (2 * k, 2 * k + 1) for tg in range(GROUPS)] for k in range(4)]
+        batches = [
+            [(n, 0) for n in range(4)],
+            [(n, 1) for n in range(4)],
+            [(n, tg) for n in (4, 5) for tg in range(2)],
+            [(n, tg) for n in (6, 7) for tg in range(2)],
+        ]
 
         def each(fn, k, lo=0, hi=4):
             for b in batches[k][lo:hi]:
@@ -309,7 +327,7 @@ def tile_bcmslidingthresholdtraceupdate_x2_kernel(
                 log(*b)
                 rate(*b)
 
-        def turns(name, tg, jp, warm=True):
+        def turns(name, tg, jp, warm):
             turn(name, tg, jp, 0, warm)
             turn(name, tg, jp, 1, warm)
 
@@ -329,73 +347,128 @@ def tile_bcmslidingthresholdtraceupdate_x2_kernel(
             store_f32(n0, n1, 0)
             store_f32(n0, n1, 1)
 
-        for tg in range(GROUPS):
-            turns("r", tg, 0, False and tg == 0)
-            turns("r", tg, 1, False)
-            quants("r", tg, 0)
-            if tg == 1:
-                both(trace_quant, 0)
-            turns("x", tg, 0, False)
-            quants("r", tg, 1)
-            turns("x", tg, 1, False)
-            quants("x", tg, 0)
-            for n in (0, 1):
-                drive(n, tg, 0, 2)
-            quants("x", tg, 1)
-            for n in (0, 1):
-                drive(n, tg, 2, 4)
-                sigmoid(n, tg)
-            both(trace_interleave, tg)
+        sort_words("r", 0, 0)
+        turns("r", 0, 0, "s")
+        sort_words("r", 0, 1)
+        late_loads()
+        turns("r", 0, 1, "s")
+        quants("r", 0, 0)
+        sort_words("x", 0, 0)
+        turns("x", 0, 0, "s")
+        quants("r", 0, 1)
+        sort_words("x", 0, 1)
+        for b in batches[0][0:2]:
+            drive(*b, 0, 2)
+        turns("x", 0, 1, "s")
+        for b in batches[0][2:4]:
+            drive(*b, 0, 2)
+        quants("x", 0, 0)
+        trace_interleave(0, 0)
+        quants("x", 0, 1)
+        for b in batches[0]:
+            drive(*b, 2, 4)
+            sigmoid(*b)
+        trace_interleave(0, 1)
+        both(trace_quant, 0)
+        turns("x", 1, 0, "n")
+        turns("x", 1, 1, "n")
+        each(log, 0)
+        turns("r", 1, 0, "s")
+        turns("r", 1, 1, "s")
+        quants("x", 1, 0)
+        each(rate, 0, 0, 1)
+        quants("x", 1, 1)
+        each(rate, 0, 1, 4)
+        quants("r", 1, 0)
+        each(slope, 0, 0, 1)
+        quants("r", 1, 1)
+        for b in batches[1]:
+            drive(*b, 0, 2)
+        for b in batches[1]:
+            drive(*b, 2, 4)
+        each(sigmoid, 1)
+        each(slope, 0, 1, 4)
+        both(trace_interleave, 1)
+        both(trace_quant, 1)
         nc.vector.tensor_scalar(out=neg_g[:], in0=g_raw[:], scalar1=-1.0, scalar2=None, op0=ALU.mult)
-        for k in range(4):
-            a, b = 2 * k, 2 * k + 1
-            last = k == 3
-            logs_and_rates(k)
-            if not last:
-                each(drive, k + 1)
-            if k > 0 and not last:
-                both(out_copy, a - 2)
-                both(out_copy, b - 2)
-                stores(a - 2, a)
-            each(square, k)
-            if last:
-                both(out_copy, a - 2)
-                both(out_copy, b - 2)
-                stores(a - 2, a)
-                both(out_cast_s, a - 2)
-                both(out_cast_s, b - 2)
-            else:
-                each(sigmoid, k + 1)
-            each(slope, k)
-            if k == 0:
-                both(trace_quant, 1)
-            elif not last:
-                both(out_cast, a - 2)
-                both(out_cast, b - 2)
-            threshold(a, b + 1)
-            if 0 < k < 3:
-                both(out_quant, a - 2)
-                both(out_quant, b - 2)
-                store_words(a - 2, a)
-            to_time(a)
-            to_time(b)
-            both(gain, a)
-            gain(b, 0)
-            stage2(a)
-            gain(b, 1)
-            if last:
-                both(out_quant, a - 2)
-                both(out_quant, b - 2)
-                store_words(a - 2, a)
-            stage2(b)
+        logs_and_rates(1)
+        each(drive, 2)
+        for n in range(4):
+            square(n)
+        each(sigmoid, 2)
+        each(slope, 1)
+        to_time(0)
+        to_time(1)
+        both(gain, 0)
+        both(bcm, 2)
+        stage2(0)
+        both(gain, 1)
+        both(bcm, 3)
+        stage2(1)
+        logs_and_rates(2)
+        both(out_copy, 0)
+        both(out_copy, 1)
+        stores(0, 2)
+        each(drive, 3, 0, 2)
+        both(turn_back, 2)
+        both(turn_back, 3)
+        each(drive, 3, 2, 4)
+        square(4)
+        square(5)
+        each(sigmoid, 3)
+        each(slope, 2)
+        both(gain, 2)
+        both(out_cast, 0)
+        stage2(2)
+        both(gain, 3)
+        both(out_quant, 0)
+        both(bcm, 4)
+        stage2(3)
+        both(out_copy, 2)
+        both(turn_back, 4)
+        both(bcm, 5)
+        both(out_cast, 1)
+        both(gain, 4)
+        both(out_quant, 1)
+        store_words(0, 2)
+        stage2(4)
+        logs_and_rates(3)
+        both(out_copy, 3)
+        stores(2, 4)
+        both(turn_back, 5)
+        square(6)
+        square(7)
+        both(slope, 6)
+        both(gain, 5)
+        both(out_copy, 4)
+        stores(4, 5)
+        both(out_cast_s, 2)
+        both(out_cast_s, 3)
+        to_time(6)
+        stage2(5)
+        both(out_copy, 5)
+        stores(5, 6)
+        both(slope, 7)
+        to_time(7)
+        both(out_quant, 2)
+        both(gain, 6)
+        both(out_quant, 3)
+        store_words(2, 4)
+        both(out_cast_psum, 4)
+        stage2(6)
+        both(gain, 7)
         both(out_copy, 6)
         stores(6, 7)
+        both(out_cast, 5)
+        stage2(7)
+        both(out_quant, 4)
+        both(out_quant, 5)
+        store_words(4, 6)
         both(out_cast, 6)
         both(out_copy, 7)
         stores(7, 8)
         both(out_quant, 6)
-        store_words(6, 7)
         both(out_cast, 7)
         both(out_quant, 7)
-        store_words(7, 8)
+        store_words(6, 8)
         store_scales()

@@ -130,8 +130,9 @@ def tile_bcmslidingthresholdtraceupdate_x2_kernel(
                         base = jj * (D // 2) + kp * 256
                         src = words[:, base + u:base + 256:2]
                     nc.tensor.transpose(bank[:, u, jj, :], src, ident[:])
-            grouped[name, tg, jp, kp] = work.tile([P, 2 * BANK], BF16, name="grouped", tag="grouped", bufs=8, align_bytes=64)
-            dst = grouped[name, tg, jp, kp][:]
+            if jp == 0:
+                grouped[name, tg, kp] = work.tile([P, 4 * BANK], BF16, name="grouped", tag="grouped", bufs=4, align_bytes=64)
+            dst = grouped[name, tg, kp][:, jp * 2 * BANK:(jp + 1) * 2 * BANK]
             if "s" in how:
                 nc.scalar.copy(out=dst.bitcast(F32).rearrange("p (c u) -> p c u", u=2),
                                in_=bank[:].rearrange("p u j t -> p (j t) u"))
@@ -143,35 +144,33 @@ def tile_bcmslidingthresholdtraceupdate_x2_kernel(
                 nc.vector.tensor_scalar(out=dst.rearrange("p (c u e) -> p c u e", u=2, e=2), in0=src,
                                         scalar1=-1.0, scalar2=None, op0=ALU.mult)
 
-        def quant_act(name, tg, jp, kp):
-            if jp == 0:
-                acode[name, tg, kp] = keep.tile([P, BANK], U32, name="acode_%s%d%d" % (name, tg, kp), align_bytes=64)
-                ascale[name, tg, kp] = keep.tile([P, BANK], U8, name="ascale_%s%d%d" % (name, tg, kp), align_bytes=64)
-            cols = slice(jp * 2 * P, (jp + 1) * 2 * P)
-            nc.vector.quantize_mx(out=acode[name, tg, kp][:, cols].bitcast(FP8X4), scales=ascale[name, tg, kp][:, cols],
-                                  in_=grouped[name, tg, jp, kp][:])
+        def quant_act(name, tg, kp):
+            acode[name, tg, kp] = keep.tile([P, BANK], U32, name="acode_%s%d%d" % (name, tg, kp), align_bytes=64)
+            ascale[name, tg, kp] = keep.tile([P, BANK], U8, name="ascale_%s%d%d" % (name, tg, kp), align_bytes=64)
+            nc.vector.quantize_mx(out=acode[name, tg, kp][:].bitcast(FP8X4), scales=ascale[name, tg, kp][:],
+                                  in_=grouped[name, tg, kp][:])
 
         tcode = {}
         tscale = {}
         tgrouped = {}
 
         def trace_interleave(tg, dg):
-            t_ = work.tile([P, 4 * BANK], BF16, name="tgrouped", tag="tgrouped", bufs=2, align_bytes=64)
+            if dg == 0:
+                tgrouped[tg] = work.tile([P, GROUPS, 4 * BANK], BF16, name="tgrouped", tag="tgrouped", bufs=1, align_bytes=64)
             nc.vector.tensor_copy(
-                out=t_[:].rearrange("p (s m j) -> p s m j", s=PACK, j=PACK),
+                out=tgrouped[tg][:, dg, :].rearrange("p (s m j) -> p s m j", s=PACK, j=PACK),
                 in_=traw[tg][:, :, dg * K_PASS:(dg + 1) * K_PASS].rearrange("p j (m s) -> p s m j", s=PACK))
-            tgrouped[tg, dg] = t_
 
-        def trace_quant(tg, dg):
-            tcode[tg, dg] = keep.tile([P, BANK], U32, name="tcode%d%d" % (tg, dg), align_bytes=64)
-            tscale[tg, dg] = keep.tile([P, BANK], U8, name="tscale%d%d" % (tg, dg), align_bytes=64)
-            nc.vector.quantize_mx(out=tcode[tg, dg][:].bitcast(FP8X4), scales=tscale[tg, dg][:], in_=tgrouped[tg, dg][:])
+        def trace_quant(tg):
+            tcode[tg] = keep.tile([P, D], U32, name="tcode%d" % tg, align_bytes=64)
+            tscale[tg] = keep.tile([P, D], U8, name="tscale%d" % tg, align_bytes=64)
+            nc.vector.quantize_mx(out=tcode[tg][:].bitcast(FP8X4), scales=tscale[tg][:], in_=tgrouped[tg][:].rearrange("p h c -> p (h c)"))
 
         zbank = {}
         sn = {}
         ln = {}
         na = {}
-        na_both = {}
+        sn_two = {}
         u_ = {}
         wv = {}
         theta = keep.tile([P, N_TILES], F32, name="theta")
@@ -195,34 +194,46 @@ def tile_bcmslidingthresholdtraceupdate_x2_kernel(
                     start=(i == 0), stop=(i == len(passes) - 1))
 
         def sigmoid(n, tg):
-            sn[n, tg] = work.tile([P, BANK], F32, name="sn", tag="sn", bufs=8)
-            nc.scalar.activation(out=sn[n, tg][:], in_=zbank[n, tg][:], func=ACT.Sigmoid)
+            key, row = ((n // 2, tg), n % 2) if n < 4 else (n, tg)
+            if row == 0:
+                sn_two[key] = work.tile([P, 2, BANK], F32, name="sn", tag="sn", bufs=4)
+            sn[n, tg] = sn_two[key][:, row, :]
+            nc.scalar.activation(out=sn[n, tg], in_=zbank[n, tg][:], func=ACT.Sigmoid)
 
         def log(n, tg):
             ln[n, tg] = work.tile([P, BANK], F32, name="ln", tag="ln", bufs=4)
-            nc.scalar.activation(out=ln[n, tg][:], in_=sn[n, tg][:], func=ACT.Ln)
+            nc.scalar.activation(out=ln[n, tg][:], in_=sn[n, tg], func=ACT.Ln)
 
         def rate(n, tg):
-            if tg == 0:
-                na_both[n] = work.tile([P, GROUPS, BANK], F32, name="na", tag="na", bufs=6)
-            na[n, tg] = na_both[n][:, tg, :]
-            nc.vector.scalar_tensor_tensor(out=na[n, tg], in0=ln[n, tg][:], scalar=-LINEAR_FROM, in1=zbank[n, tg][:],
-                                           op0=ALU.max, op1=ALU.min)
+            if tg == 0 and n % 2 == 0:
+                na[n // 2] = work.tile([P, 2, GROUPS, BANK], F32, name="na", tag="na", bufs=3)
+            nc.vector.scalar_tensor_tensor(out=na[n // 2][:, n % 2, tg, :], in0=ln[n, tg][:], scalar=-LINEAR_FROM,
+                                           in1=zbank[n, tg][:], op0=ALU.max, op1=ALU.min)
+
+        def row_of(pairs, n):
+            return pairs[n // 2][:, n % 2, :, :].rearrange("p g t -> p (g t)")
 
         def square(n):
             junk = work.tile([P, T], BF16, name="junk", tag="junk", bufs=1)
-            nc.scalar.activation(out=junk[:], in_=na_both[n][:].rearrange("p g t -> p (g t)"), func=ACT.Square,
+            nc.scalar.activation(out=junk[:], in_=row_of(na, n), func=ACT.Square,
                                  scale=INV_SQRT_T, accum_out=theta[:, n:n + 1])
 
-        def slope(n, tg):
-            u_[n, tg] = work.tile([P, BANK], F32, name="u", tag="u", bufs=12)
-            nc.vector.scalar_tensor_tensor(out=u_[n, tg][:], in0=sn[n, tg][:], scalar=1.0, in1=na[n, tg],
+        def slope_half(q, tg):
+            if tg == 0:
+                u_[q] = work.tile([P, 2, GROUPS, BANK], F32, name="u", tag="u", bufs=3)
+            nc.vector.scalar_tensor_tensor(out=u_[q][:, :, tg, :], in0=sn_two[q, tg][:], scalar=1.0, in1=na[q][:, :, tg, :],
                                            op0=ALU.subtract, op1=ALU.mult)
 
-        def bcm(n, tg):
-            wv[n, tg] = work.tile([P, BANK], F32, name="wv", tag="wv", bufs=4)
-            nc.vector.scalar_tensor_tensor(out=wv[n, tg][:], in0=na[n, tg], scalar=theta[:, n:n + 1], in1=u_[n, tg][:],
-                                           op0=ALU.add, op1=ALU.mult)
+        def slope(n):
+            if n % 2 == 0:
+                u_[n // 2] = work.tile([P, 2, GROUPS, BANK], F32, name="u", tag="u", bufs=3)
+            nc.vector.scalar_tensor_tensor(out=row_of(u_, n), in0=sn_two[n][:].rearrange("p g t -> p (g t)"), scalar=1.0,
+                                           in1=row_of(na, n), op0=ALU.subtract, op1=ALU.mult)
+
+        def bcm(n):
+            wv[n] = work.tile([P, T], F32, name="wv", tag="wv", bufs=2)
+            nc.vector.scalar_tensor_tensor(out=wv[n][:], in0=row_of(na, n), scalar=theta[:, n:n + 1],
+                                           in1=row_of(u_, n), op0=ALU.add, op1=ALU.mult)
 
         def pair_of(n):
             return 2 * (n % 2) + (4 if n < 6 else 0)
@@ -235,7 +246,7 @@ def tile_bcmslidingthresholdtraceupdate_x2_kernel(
         def turn_back(n, tg):
             bank = psum.tile([P, PACK, P], F32, name="pbank", tag="bank%d" % (pair_of(n) + tg))
             for j in range(PACK):
-                nc.tensor.transpose(bank[:, j, :], wv[n, tg][:, j * P:(j + 1) * P], ident[:])
+                nc.tensor.transpose(bank[:, j, :], wv[n][:, tg * BANK + j * P:tg * BANK + (j + 1) * P], ident[:])
             pbank[n, tg] = bank
 
         def gain(n, tg):
@@ -262,8 +273,8 @@ def tile_bcmslidingthresholdtraceupdate_x2_kernel(
                 for tg in range(GROUPS):
                     nc.tensor.matmul_mx(
                         out=bank[:, s, :],
-                        lhsT=tcode[tg, dg][:, s * P:(s + 1) * P].bitcast(FP8X4),
-                        lhsT_scale=tscale[tg, dg][:, s * P:(s + 1) * P],
+                        lhsT=tcode[tg][:, dg * BANK + s * P:dg * BANK + (s + 1) * P].bitcast(FP8X4),
+                        lhsT_scale=tscale[tg][:, dg * BANK + s * P:dg * BANK + (s + 1) * P],
                         rhs=pcode[n][:, tg * P:(tg + 1) * P].bitcast(FP8X4),
                         rhs_scale=pscale[n][:, tg * P:(tg + 1) * P],
                         start=(tg == 0), stop=(tg == GROUPS - 1))
@@ -275,23 +286,18 @@ def tile_bcmslidingthresholdtraceupdate_x2_kernel(
             c0 = (n % 2) * P
             nc.scalar.activation(out=of32[n // 2, dg][:, :, c0:c0 + P], in_=obank[n, dg][:], func=ACT.Copy, scale=INV_SQRT_T)
 
-        def out_cast(n, dg):
-            obf[n, dg] = work.tile([P, P, PACK], BF16, name="obf", tag="obf", bufs=4, align_bytes=64)
-            c0 = (n % 2) * P
-            nc.vector.tensor_copy(out=obf[n, dg][:], in_=of32[n // 2, dg][:, :, c0:c0 + P].rearrange("p s n -> p n s"))
+        def out_cast(n0, n1, dg, engine):
+            obf[n0, dg] = work.tile([P, (n1 - n0) * P, PACK], BF16, name="obf", tag="obf", bufs=4, align_bytes=64)
+            c0 = (n0 % 2) * P
+            src = of32[n0 // 2, dg][:, :, c0:c0 + (n1 - n0) * P].rearrange("p s n -> p n s")
+            if engine == "s":
+                nc.scalar.copy(out=obf[n0, dg][:], in_=src)
+            else:
+                nc.vector.tensor_copy(out=obf[n0, dg][:], in_=src)
 
-        def out_quant(n, dg):
-            nc.vector.quantize_mx(out=ocode[:, dg, n * P:(n + 1) * P].bitcast(FP8X4), scales=oscale[:, dg, n * P:(n + 1) * P],
-                                  in_=obf[n, dg][:].rearrange("p n s -> p (n s)"))
-
-        def out_cast_psum(n, dg):
-            obf[n, dg] = work.tile([P, P, PACK], BF16, name="obf", tag="obf", bufs=4, align_bytes=64)
-            nc.scalar.activation(out=obf[n, dg][:], in_=obank[n, dg][:].rearrange("p s n -> p n s"), func=ACT.Copy, scale=INV_SQRT_T)
-
-        def out_cast_s(n, dg):
-            obf[n, dg] = work.tile([P, P, PACK], BF16, name="obf", tag="obf", bufs=4, align_bytes=64)
-            c0 = (n % 2) * P
-            nc.scalar.copy(out=obf[n, dg][:], in_=of32[n // 2, dg][:, :, c0:c0 + P].rearrange("p s n -> p n s"))
+        def out_quant(n0, n1, dg):
+            nc.vector.quantize_mx(out=ocode[:, dg, n0 * P:n1 * P].bitcast(FP8X4), scales=oscale[:, dg, n0 * P:n1 * P],
+                                  in_=obf[n0, dg][:].rearrange("p n s -> p (n s)"))
 
         def store_f32(n0, n1, dg):
             rows = out_0[dg * K_PASS:(dg + 1) * K_PASS, n0 * P:n1 * P].rearrange("(p s) n -> p s n", s=PACK)
@@ -331,12 +337,20 @@ def tile_bcmslidingthresholdtraceupdate_x2_kernel(
             turn(name, tg, jp, 0, warm)
             turn(name, tg, jp, 1, warm)
 
-        def quants(name, tg, jp):
-            quant_act(name, tg, jp, 0)
-            quant_act(name, tg, jp, 1)
+        def quants(name, tg):
+            quant_act(name, tg, 0)
+            quant_act(name, tg, 1)
+
+        def casts(n0, n1, engine):
+            out_cast(n0, n1, 0, engine)
+            out_cast(n0, n1, 1, engine)
+
+        def out_quants(n0, n1):
+            out_quant(n0, n1, 0)
+            out_quant(n0, n1, 1)
 
         def to_time(n):
-            both(bcm, n)
+            bcm(n)
             both(turn_back, n)
 
         def stage2(n):
@@ -352,58 +366,53 @@ def tile_bcmslidingthresholdtraceupdate_x2_kernel(
         sort_words("r", 0, 1)
         late_loads()
         turns("r", 0, 1, "s")
-        quants("r", 0, 0)
         sort_words("x", 0, 0)
         turns("x", 0, 0, "s")
-        quants("r", 0, 1)
+        quant_act("r", 0, 0)
         sort_words("x", 0, 1)
-        for b in batches[0][0:2]:
-            drive(*b, 0, 2)
+        quant_act("r", 0, 1)
         turns("x", 0, 1, "s")
-        for b in batches[0][2:4]:
+        for b in batches[0]:
             drive(*b, 0, 2)
-        quants("x", 0, 0)
-        trace_interleave(0, 0)
-        quants("x", 0, 1)
+        quants("x", 0)
         for b in batches[0]:
             drive(*b, 2, 4)
             sigmoid(*b)
-        trace_interleave(0, 1)
-        both(trace_quant, 0)
+        both(trace_interleave, 0)
+        trace_quant(0)
         turns("x", 1, 0, "n")
         turns("x", 1, 1, "n")
         each(log, 0)
         turns("r", 1, 0, "s")
         turns("r", 1, 1, "s")
-        quants("x", 1, 0)
         each(rate, 0, 0, 1)
-        quants("x", 1, 1)
+        quants("x", 1)
         each(rate, 0, 1, 4)
-        quants("r", 1, 0)
-        each(slope, 0, 0, 1)
-        quants("r", 1, 1)
         for b in batches[1]:
             drive(*b, 0, 2)
+        quants("r", 1)
         for b in batches[1]:
             drive(*b, 2, 4)
         each(sigmoid, 1)
-        each(slope, 0, 1, 4)
+        slope_half(0, 0)
+        slope_half(1, 0)
         both(trace_interleave, 1)
-        both(trace_quant, 1)
         nc.vector.tensor_scalar(out=neg_g[:], in0=g_raw[:], scalar1=-1.0, scalar2=None, op0=ALU.mult)
+        trace_quant(1)
         logs_and_rates(1)
         each(drive, 2)
         for n in range(4):
             square(n)
         each(sigmoid, 2)
-        each(slope, 1)
+        slope_half(0, 1)
+        slope_half(1, 1)
         to_time(0)
         to_time(1)
         both(gain, 0)
-        both(bcm, 2)
+        bcm(2)
         stage2(0)
         both(gain, 1)
-        both(bcm, 3)
+        bcm(3)
         stage2(1)
         logs_and_rates(2)
         both(out_copy, 0)
@@ -416,20 +425,20 @@ def tile_bcmslidingthresholdtraceupdate_x2_kernel(
         square(4)
         square(5)
         each(sigmoid, 3)
-        each(slope, 2)
+        slope(4)
+        slope(5)
         both(gain, 2)
-        both(out_cast, 0)
+        out_cast(0, 2, 0, "v")
         stage2(2)
         both(gain, 3)
-        both(out_quant, 0)
-        both(bcm, 4)
+        bcm(4)
         stage2(3)
         both(out_copy, 2)
         both(turn_back, 4)
-        both(bcm, 5)
-        both(out_cast, 1)
+        bcm(5)
+        out_cast(0, 2, 1, "v")
         both(gain, 4)
-        both(out_quant, 1)
+        out_quants(0, 2)
         store_words(0, 2)
         stage2(4)
         logs_and_rates(3)
@@ -438,37 +447,34 @@ def tile_bcmslidingthresholdtraceupdate_x2_kernel(
         both(turn_back, 5)
         square(6)
         square(7)
-        both(slope, 6)
+        slope(6)
         both(gain, 5)
         both(out_copy, 4)
         stores(4, 5)
-        both(out_cast_s, 2)
-        both(out_cast_s, 3)
+        casts(2, 4, "s")
         to_time(6)
         stage2(5)
+        slope(7)
         both(out_copy, 5)
         stores(5, 6)
-        both(slope, 7)
-        to_time(7)
-        both(out_quant, 2)
         both(gain, 6)
-        both(out_quant, 3)
-        store_words(2, 4)
-        both(out_cast_psum, 4)
+        to_time(7)
         stage2(6)
-        both(gain, 7)
+        out_quants(2, 4)
+        store_words(2, 4)
         both(out_copy, 6)
         stores(6, 7)
-        both(out_cast, 5)
+        both(gain, 7)
+        out_cast(4, 6, 0, "v")
         stage2(7)
-        both(out_quant, 4)
-        both(out_quant, 5)
+        out_cast(4, 6, 1, "v")
+        casts(6, 7, "s")
+        out_quants(4, 6)
         store_words(4, 6)
-        both(out_cast, 6)
+        out_quants(6, 7)
         both(out_copy, 7)
         stores(7, 8)
-        both(out_quant, 6)
-        both(out_cast, 7)
-        both(out_quant, 7)
+        casts(7, 8, "v")
+        out_quants(7, 8)
         store_words(6, 8)
         store_scales()

@@ -22,6 +22,9 @@ K_PASS = P * PACK
 GROUPS = 2
 N_TILES = N // P
 BANK = 512
+DRIVE_BANKS = 4
+SPLIT_TILES = 4
+LATE_TILES = 6
 LINEAR_FROM = 20.0
 INV_SQRT_T = 1.0 / 32.0
 
@@ -36,113 +39,105 @@ def tile_bcmslidingthresholdtraceupdate_x2_kernel(
         psum = ctx.enter_context(tc.psum_pool(name="psum", bufs=1))
         ctx.enter_context(tc.manual_schedule())
 
-        warm_in = keep.tile([P, 1], F32, name="warm_in")
-        warm_out = keep.tile([P, 1], F32, name="warm_out")
-        nc.vector.memset(warm_in[:], 0.0)
-        nc.scalar.activation(out=warm_out[:], in_=warm_in[:], func=ACT.Sigmoid)
-
         ident = keep.tile([P, P], F32, name="ident")
         make_identity(nc, ident[:])
 
         wscale = {}
-        for name in ("w", "l"):
-            wscale[name] = keep.tile([P, GROUPS, N], U8, name=name + "_scale", align_bytes=64)
-            nc.vector.memset(wscale[name][:].rearrange("p g n -> p (g n)").bitcast(I32), 0)
+        for uh in range(2):
+            for name in ("l", "w"):
+                wscale[name, uh] = keep.tile([P, GROUPS, BANK], U8, name="scale_%s%d" % (name, uh), align_bytes=64)
+                nc.vector.memset(wscale[name, uh][:].rearrange("p g n -> p (g n)").bitcast(I32), 0)
 
         act_src = {"x": x, "r": r}
+        words_src = {"w": w_words, "l": l_words}
+        scales_src = {"w": w_scales, "l": l_scales}
         raw = {}
-
-        def load_act(name, tg, jp):
-            t_ = work.tile([P, 2, D], BF16, name="raw", tag="raw", bufs=6, align_bytes=64)
-            rows = act_src[name][tg * K_PASS:(tg + 1) * K_PASS, :].rearrange("(p j) k -> p j k", j=PACK)
-            nc.sync.dma_start(out=t_[:], in_=rows[:, 2 * jp:2 * jp + 2, :])
-            raw[name, tg, jp] = t_
-
-        w_src = {"w": w_words, "l": l_words}
-        s_src = {"w": w_scales, "l": l_scales}
         wcode = {}
-
-        def load_words(name, half):
-            t_ = keep.tile([P, GROUPS, N], U8, name="words_%s%d" % (name, half), align_bytes=64)
-            src = w_src[name][:, :, half * N:(half + 1) * N].rearrange("g p b -> p g b")
-            nc.sync.dma_start(out=t_[:].bitcast(I32), in_=src.bitcast(I32))
-            wcode[name, half] = t_
-
-        def load_scales(name):
-            for q in range(4):
-                src = s_src[name][:, 4 * q:4 * q + 4, :].rearrange("g r n -> r g n")
-                nc.sync.dma_start(out=wscale[name][32 * q:32 * q + 4, :, :].bitcast(I32), in_=src.bitcast(I32))
-
         traw = {}
 
+        def load_act(name, tg, jp):
+            raw[name, tg, jp] = work.tile([P, 2, D], BF16, name="raw", tag="raw", bufs=6, align_bytes=64)
+            rows = act_src[name][tg * K_PASS:(tg + 1) * K_PASS, :].rearrange("(p j) k -> p j k", j=PACK)
+            nc.sync.dma_start(out=raw[name, tg, jp][:], in_=rows[:, 2 * jp:2 * jp + 2, :])
+
+        def load_words(name, uh):
+            wcode[name, uh] = keep.tile([P, GROUPS, N], U8, name="words_%s%d" % (name, uh), align_bytes=64)
+            src = words_src[name][:, :, uh * N:(uh + 1) * N].rearrange("g p b -> p g b")
+            nc.sync.dma_start(out=wcode[name, uh][:].bitcast(I32), in_=src.bitcast(I32))
+
+        def load_scales(name, uh):
+            for i in range(4):
+                src = scales_src[name][:, i:16:4, uh * BANK:(uh + 1) * BANK].rearrange("g q n -> q g n")
+                nc.sync.dma_start(out=wscale[name, uh][i:P:32, :, :].bitcast(I32), in_=src.bitcast(I32))
+
         def load_trace(tg):
-            t_ = keep.tile([P, PACK, D], BF16, name="traw%d" % tg, align_bytes=64)
-            nc.sync.dma_start(out=t_[:], in_=trace[tg * K_PASS:(tg + 1) * K_PASS, :].rearrange("(p j) d -> p j d", j=PACK))
-            traw[tg] = t_
+            traw[tg] = keep.tile([P, PACK, D], BF16, name="traw%d" % tg, align_bytes=64)
+            rows = trace[tg * K_PASS:(tg + 1) * K_PASS, :].rearrange("(p j) d -> p j d", j=PACK)
+            nc.sync.dma_start(out=traw[tg][:], in_=rows)
 
         load_act("r", 0, 0)
         load_act("r", 0, 1)
-        load_scales("l")
+        load_scales("l", 0)
         load_words("l", 0)
         load_act("x", 0, 0)
         load_act("x", 0, 1)
-        load_scales("w")
+        load_scales("w", 0)
         load_words("w", 0)
         load_trace(0)
         load_act("x", 1, 0)
         load_act("x", 1, 1)
         g_raw = keep.tile([P, GROUPS, PACK], BF16, name="g_raw")
 
-        def late_loads():
+        def remaining_loads():
             load_act("r", 1, 0)
             load_act("r", 1, 1)
             load_trace(1)
             load_words("l", 1)
             load_words("w", 1)
+            load_scales("l", 1)
+            load_scales("w", 1)
             nc.sync.dma_start(out=g_raw[:], in_=g.rearrange("(g p j) -> p g j", g=GROUPS, j=PACK))
 
+        sorted_pairs = {}
         grouped = {}
         acode = {}
         ascale = {}
 
-        halves = {}
-
-        def sort_words(name, tg, jp):
-            halves[name, tg, jp] = work.tile([P, 4, 2, P], F32, name="halves", tag="halves", bufs=2)
+        def sort_pairs(name, tg, jp):
+            sorted_pairs[name, tg, jp] = work.tile([P, 4, 2, P], F32, name="sorted_pairs", tag="sorted_pairs", bufs=2)
+            dst = sorted_pairs[name, tg, jp]
             rows = raw[name, tg, jp][:].rearrange("p j k -> p (j k)")
             if name == "r":
-                nc.vector.tensor_copy(out=halves[name, tg, jp][:],
-                                      in_=rows.bitcast(F32).rearrange("p (c q u) -> p c u q", c=4, u=2))
+                nc.vector.tensor_copy(out=dst[:], in_=rows.bitcast(F32).rearrange("p (c q u) -> p c u q", c=4, u=2))
             else:
                 src = rows.rearrange("p (c q u e) -> p c u q e", c=4, u=2, e=2)
                 for u in range(2):
-                    dst = halves[name, tg, jp][:, :, u, :].bitcast(BF16).rearrange("p c (q e) -> p c q e", e=2)
-                    nc.vector.tensor_scalar(out=dst, in0=src[:, :, u, :, :], scalar1=-1.0, scalar2=None, op0=ALU.mult)
+                    nc.vector.tensor_scalar(
+                        out=dst[:, :, u, :].bitcast(BF16).rearrange("p c (q e) -> p c q e", e=2),
+                        in0=src[:, :, u, :, :], scalar1=-1.0, scalar2=None, op0=ALU.mult)
 
-        def turn(name, tg, jp, kp, how):
-            bank = psum.tile([P, 2, 2, P], F32, name="tbank", tag="bank%d" % (4 + 2 * jp + kp))
-            words = raw[name, tg, jp][:].rearrange("p j k -> p (j k)").bitcast(F32)
+        def turn(name, tg, jp, kp):
+            bank = psum.tile([P, 2, 2, P], F32, name="tbank", tag="bank%d" % (DRIVE_BANKS + 2 * jp + kp))
+            pairs = raw[name, tg, jp][:].rearrange("p j k -> p (j k)").bitcast(F32)
             for jj in range(2):
                 for u in range(2):
-                    if (name, tg, jp) in halves:
-                        src = halves[name, tg, jp][:, 2 * jj + kp, u, :]
+                    if tg == 0:
+                        src = sorted_pairs[name, tg, jp][:, 2 * jj + kp, u, :]
                     else:
-                        base = jj * (D // 2) + kp * 256
-                        src = words[:, base + u:base + 256:2]
+                        base = jj * (D // 2) + kp * 2 * P
+                        src = pairs[:, base + u:base + 2 * P:2]
                     nc.tensor.transpose(bank[:, u, jj, :], src, ident[:])
             if jp == 0:
-                grouped[name, tg, kp] = work.tile([P, 4 * BANK], BF16, name="grouped", tag="grouped", bufs=4, align_bytes=64)
+                grouped[name, tg, kp] = work.tile([P, PACK * BANK], BF16, name="grouped", tag="grouped", bufs=4,
+                                                  align_bytes=64)
             dst = grouped[name, tg, kp][:, jp * 2 * BANK:(jp + 1) * 2 * BANK]
-            if "s" in how:
-                nc.scalar.copy(out=dst.bitcast(F32).rearrange("p (c u) -> p c u", u=2),
-                               in_=bank[:].rearrange("p u j t -> p (j t) u"))
-            elif "v" in how:
-                nc.vector.tensor_copy(out=dst.bitcast(F32).rearrange("p (c u) -> p c u", u=2),
-                                      in_=bank[:].rearrange("p u j t -> p (j t) u"))
-            else:
+            if name == "x" and tg == 1:
                 src = bank[:].rearrange("p u j t -> p (u j t)").bitcast(BF16).rearrange("p (u c e) -> p c u e", u=2, e=2)
                 nc.vector.tensor_scalar(out=dst.rearrange("p (c u e) -> p c u e", u=2, e=2), in0=src,
                                         scalar1=-1.0, scalar2=None, op0=ALU.mult)
+            else:
+                nc.scalar.copy(out=dst.bitcast(F32).rearrange("p (c u) -> p c u", u=2),
+                               in_=bank[:].rearrange("p u j t -> p (j t) u"))
 
         def quant_act(name, tg, kp):
             acode[name, tg, kp] = keep.tile([P, BANK], U32, name="acode_%s%d%d" % (name, tg, kp), align_bytes=64)
@@ -150,13 +145,14 @@ def tile_bcmslidingthresholdtraceupdate_x2_kernel(
             nc.vector.quantize_mx(out=acode[name, tg, kp][:].bitcast(FP8X4), scales=ascale[name, tg, kp][:],
                                   in_=grouped[name, tg, kp][:])
 
+        tgrouped = {}
         tcode = {}
         tscale = {}
-        tgrouped = {}
 
         def trace_interleave(tg, dg):
             if dg == 0:
-                tgrouped[tg] = work.tile([P, GROUPS, 4 * BANK], BF16, name="tgrouped", tag="tgrouped", bufs=1, align_bytes=64)
+                tgrouped[tg] = work.tile([P, GROUPS, PACK * BANK], BF16, name="tgrouped", tag="tgrouped", bufs=1,
+                                         align_bytes=64)
             nc.vector.tensor_copy(
                 out=tgrouped[tg][:, dg, :].rearrange("p (s m j) -> p s m j", s=PACK, j=PACK),
                 in_=traw[tg][:, :, dg * K_PASS:(dg + 1) * K_PASS].rearrange("p j (m s) -> p s m j", s=PACK))
@@ -164,79 +160,81 @@ def tile_bcmslidingthresholdtraceupdate_x2_kernel(
         def trace_quant(tg):
             tcode[tg] = keep.tile([P, D], U32, name="tcode%d" % tg, align_bytes=64)
             tscale[tg] = keep.tile([P, D], U8, name="tscale%d" % tg, align_bytes=64)
-            nc.vector.quantize_mx(out=tcode[tg][:].bitcast(FP8X4), scales=tscale[tg][:], in_=tgrouped[tg][:].rearrange("p h c -> p (h c)"))
+            nc.vector.quantize_mx(out=tcode[tg][:].bitcast(FP8X4), scales=tscale[tg][:],
+                                  in_=tgrouped[tg][:].rearrange("p h c -> p (h c)"))
 
         zbank = {}
-        sn = {}
-        ln = {}
-        na = {}
-        sn_two = {}
-        u_ = {}
-        wv = {}
+        q_two = {}
+        q_one = {}
+        log_q = {}
+        neg_a = {}
+        slope_a = {}
+        neg_phi = {}
         theta = keep.tile([P, N_TILES], F32, name="theta")
         neg_g = keep.tile([P, GROUPS, PACK], F32, name="neg_g")
 
-        pair_order = {0: (("r", "l"), ("x", "w")), 1: (("x", "w"), ("r", "l"))}
+        product_order = {0: (("r", "l"), ("x", "w")), 1: (("x", "w"), ("r", "l"))}
 
-        def drive(n, tg, i0=0, i1=4):
-            if i0 == 0:
-                zbank[n, tg] = psum.tile([P, BANK], F32, name="zbank", tag="bank%d" % (n if n < 4 else 2 * (n % 2) + tg))
-            half, col = divmod(n, 4)
-            passes = [(a_name, w_name, kp) for a_name, w_name in pair_order[tg] for kp in range(2)]
-            for i in range(i0, i1):
+        def drive(n, tg, first=0, last=4):
+            if first == 0:
+                bank = n if n < SPLIT_TILES else 2 * (n % 2) + tg
+                zbank[n, tg] = psum.tile([P, BANK], F32, name="zbank", tag="bank%d" % bank)
+            uh, col = divmod(n, N_TILES // 2)
+            passes = [(a_name, w_name, kp) for a_name, w_name in product_order[tg] for kp in range(GROUPS)]
+            for i in range(first, last):
                 a_name, w_name, kp = passes[i]
                 nc.tensor.matmul_mx(
                     out=zbank[n, tg][:],
-                    lhsT=wcode[w_name, half][:, kp, col * 2 * P:(col + 1) * 2 * P].bitcast(FP4X4),
-                    lhsT_scale=wscale[w_name][:, kp, n * P:(n + 1) * P],
+                    lhsT=wcode[w_name, uh][:, kp, col * 2 * P:(col + 1) * 2 * P].bitcast(FP4X4),
+                    lhsT_scale=wscale[w_name, uh][:, kp, col * P:(col + 1) * P],
                     rhs=acode[a_name, tg, kp][:].bitcast(FP8X4),
                     rhs_scale=ascale[a_name, tg, kp][:],
                     start=(i == 0), stop=(i == len(passes) - 1))
 
         def sigmoid(n, tg):
-            key, row = ((n // 2, tg), n % 2) if n < 4 else (n, tg)
+            key, row = ((n // 2, tg), n % 2) if n < SPLIT_TILES else (n, tg)
             if row == 0:
-                sn_two[key] = work.tile([P, 2, BANK], F32, name="sn", tag="sn", bufs=4)
-            sn[n, tg] = sn_two[key][:, row, :]
-            nc.scalar.activation(out=sn[n, tg], in_=zbank[n, tg][:], func=ACT.Sigmoid)
+                q_two[key] = work.tile([P, 2, BANK], F32, name="q_two", tag="q_two", bufs=4)
+            q_one[n, tg] = q_two[key][:, row, :]
+            nc.scalar.activation(out=q_one[n, tg], in_=zbank[n, tg][:], func=ACT.Sigmoid)
 
         def log(n, tg):
-            ln[n, tg] = work.tile([P, BANK], F32, name="ln", tag="ln", bufs=4)
-            nc.scalar.activation(out=ln[n, tg][:], in_=sn[n, tg], func=ACT.Ln)
+            log_q[n, tg] = work.tile([P, BANK], F32, name="log_q", tag="log_q", bufs=4)
+            nc.scalar.activation(out=log_q[n, tg][:], in_=q_one[n, tg], func=ACT.Ln)
 
         def rate(n, tg):
             if tg == 0 and n % 2 == 0:
-                na[n // 2] = work.tile([P, 2, GROUPS, BANK], F32, name="na", tag="na", bufs=3)
-            nc.vector.scalar_tensor_tensor(out=na[n // 2][:, n % 2, tg, :], in0=ln[n, tg][:], scalar=-LINEAR_FROM,
+                neg_a[n // 2] = work.tile([P, 2, GROUPS, BANK], F32, name="neg_a", tag="neg_a", bufs=3)
+            nc.vector.scalar_tensor_tensor(out=neg_a[n // 2][:, n % 2, tg, :], in0=log_q[n, tg][:], scalar=-LINEAR_FROM,
                                            in1=zbank[n, tg][:], op0=ALU.max, op1=ALU.min)
 
-        def row_of(pairs, n):
-            return pairs[n // 2][:, n % 2, :, :].rearrange("p g t -> p (g t)")
+        def all_time(of_pairs, n):
+            return of_pairs[n // 2][:, n % 2, :, :].rearrange("p g t -> p (g t)")
 
-        def square(n):
-            junk = work.tile([P, T], BF16, name="junk", tag="junk", bufs=1)
-            nc.scalar.activation(out=junk[:], in_=row_of(na, n), func=ACT.Square,
+        def threshold(n):
+            squares = work.tile([P, T], BF16, name="squares", tag="squares", bufs=1)
+            nc.scalar.activation(out=squares[:], in_=all_time(neg_a, n), func=ACT.Square,
                                  scale=INV_SQRT_T, accum_out=theta[:, n:n + 1])
 
-        def slope_half(q, tg):
+        def slope_of_pair(pair, tg):
             if tg == 0:
-                u_[q] = work.tile([P, 2, GROUPS, BANK], F32, name="u", tag="u", bufs=3)
-            nc.vector.scalar_tensor_tensor(out=u_[q][:, :, tg, :], in0=sn_two[q, tg][:], scalar=1.0, in1=na[q][:, :, tg, :],
-                                           op0=ALU.subtract, op1=ALU.mult)
+                slope_a[pair] = work.tile([P, 2, GROUPS, BANK], F32, name="slope_a", tag="slope_a", bufs=3)
+            nc.vector.scalar_tensor_tensor(out=slope_a[pair][:, :, tg, :], in0=q_two[pair, tg][:], scalar=1.0,
+                                           in1=neg_a[pair][:, :, tg, :], op0=ALU.subtract, op1=ALU.mult)
 
         def slope(n):
             if n % 2 == 0:
-                u_[n // 2] = work.tile([P, 2, GROUPS, BANK], F32, name="u", tag="u", bufs=3)
-            nc.vector.scalar_tensor_tensor(out=row_of(u_, n), in0=sn_two[n][:].rearrange("p g t -> p (g t)"), scalar=1.0,
-                                           in1=row_of(na, n), op0=ALU.subtract, op1=ALU.mult)
+                slope_a[n // 2] = work.tile([P, 2, GROUPS, BANK], F32, name="slope_a", tag="slope_a", bufs=3)
+            nc.vector.scalar_tensor_tensor(out=all_time(slope_a, n), in0=q_two[n][:].rearrange("p g t -> p (g t)"),
+                                           scalar=1.0, in1=all_time(neg_a, n), op0=ALU.subtract, op1=ALU.mult)
 
         def bcm(n):
-            wv[n] = work.tile([P, T], F32, name="wv", tag="wv", bufs=2)
-            nc.vector.scalar_tensor_tensor(out=wv[n][:], in0=row_of(na, n), scalar=theta[:, n:n + 1],
-                                           in1=row_of(u_, n), op0=ALU.add, op1=ALU.mult)
+            neg_phi[n] = work.tile([P, T], F32, name="neg_phi", tag="neg_phi", bufs=2)
+            nc.vector.scalar_tensor_tensor(out=neg_phi[n][:], in0=all_time(neg_a, n), scalar=theta[:, n:n + 1],
+                                           in1=all_time(slope_a, n), op0=ALU.add, op1=ALU.mult)
 
-        def pair_of(n):
-            return 2 * (n % 2) + (4 if n < 6 else 0)
+        def banks_of(n):
+            return 2 * (n % 2) + (DRIVE_BANKS if n < LATE_TILES else 0)
 
         pbank = {}
         pm = {}
@@ -244,10 +242,10 @@ def tile_bcmslidingthresholdtraceupdate_x2_kernel(
         pscale = {}
 
         def turn_back(n, tg):
-            bank = psum.tile([P, PACK, P], F32, name="pbank", tag="bank%d" % (pair_of(n) + tg))
+            pbank[n, tg] = psum.tile([P, PACK, P], F32, name="pbank", tag="bank%d" % (banks_of(n) + tg))
             for j in range(PACK):
-                nc.tensor.transpose(bank[:, j, :], wv[n][:, tg * BANK + j * P:tg * BANK + (j + 1) * P], ident[:])
-            pbank[n, tg] = bank
+                nc.tensor.transpose(pbank[n, tg][:, j, :], neg_phi[n][:, tg * BANK + j * P:tg * BANK + (j + 1) * P],
+                                    ident[:])
 
         def gain(n, tg):
             if tg == 0:
@@ -262,94 +260,79 @@ def tile_bcmslidingthresholdtraceupdate_x2_kernel(
                                   in_=pm[n][:].rearrange("p g n j -> p (g n j)"))
 
         obank = {}
-        of32 = {}
-        obf = {}
+        result = {}
+        rounded = {}
         ocode = keep.tile([P, GROUPS, N], U32, name="ocode", align_bytes=64)
         oscale = keep.tile([P, GROUPS, N], U8, name="oscale", align_bytes=64)
 
         def correlate(n, dg):
-            bank = psum.tile([P, PACK, P], F32, name="obank", tag="bank%d" % (pair_of(n) + dg))
+            obank[n, dg] = psum.tile([P, PACK, P], F32, name="obank", tag="bank%d" % (banks_of(n) + dg))
             for s in range(PACK):
+                cols = slice(dg * BANK + s * P, dg * BANK + (s + 1) * P)
                 for tg in range(GROUPS):
                     nc.tensor.matmul_mx(
-                        out=bank[:, s, :],
-                        lhsT=tcode[tg][:, dg * BANK + s * P:dg * BANK + (s + 1) * P].bitcast(FP8X4),
-                        lhsT_scale=tscale[tg][:, dg * BANK + s * P:dg * BANK + (s + 1) * P],
+                        out=obank[n, dg][:, s, :],
+                        lhsT=tcode[tg][:, cols].bitcast(FP8X4),
+                        lhsT_scale=tscale[tg][:, cols],
                         rhs=pcode[n][:, tg * P:(tg + 1) * P].bitcast(FP8X4),
                         rhs_scale=pscale[n][:, tg * P:(tg + 1) * P],
                         start=(tg == 0), stop=(tg == GROUPS - 1))
-            obank[n, dg] = bank
 
-        def out_copy(n, dg):
+        def result_cols(n0, n1):
+            return slice((n0 % 2) * P, (n0 % 2 + n1 - n0) * P)
+
+        def copy_result(n, dg):
             if n % 2 == 0:
-                of32[n // 2, dg] = work.tile([P, PACK, 2 * P], F32, name="of32", tag="of32", bufs=4)
-            c0 = (n % 2) * P
-            nc.scalar.activation(out=of32[n // 2, dg][:, :, c0:c0 + P], in_=obank[n, dg][:], func=ACT.Copy, scale=INV_SQRT_T)
+                result[n // 2, dg] = work.tile([P, PACK, 2 * P], F32, name="result", tag="result", bufs=4)
+            nc.scalar.activation(out=result[n // 2, dg][:, :, result_cols(n, n + 1)], in_=obank[n, dg][:],
+                                 func=ACT.Copy, scale=INV_SQRT_T)
 
-        def out_cast(n0, n1, dg, engine):
-            obf[n0, dg] = work.tile([P, (n1 - n0) * P, PACK], BF16, name="obf", tag="obf", bufs=4, align_bytes=64)
-            c0 = (n0 % 2) * P
-            src = of32[n0 // 2, dg][:, :, c0:c0 + (n1 - n0) * P].rearrange("p s n -> p n s")
-            if engine == "s":
-                nc.scalar.copy(out=obf[n0, dg][:], in_=src)
-            else:
-                nc.vector.tensor_copy(out=obf[n0, dg][:], in_=src)
+        def round_result(n0, n1, dg, copy):
+            rounded[n0, dg] = work.tile([P, (n1 - n0) * P, PACK], BF16, name="rounded", tag="rounded", bufs=4,
+                                        align_bytes=64)
+            copy(out=rounded[n0, dg][:], in_=result[n0 // 2, dg][:, :, result_cols(n0, n1)].rearrange("p s n -> p n s"))
 
-        def out_quant(n0, n1, dg):
-            nc.vector.quantize_mx(out=ocode[:, dg, n0 * P:n1 * P].bitcast(FP8X4), scales=oscale[:, dg, n0 * P:n1 * P],
-                                  in_=obf[n0, dg][:].rearrange("p n s -> p (n s)"))
+        def quant_result(n0, n1):
+            for dg in range(GROUPS):
+                nc.vector.quantize_mx(out=ocode[:, dg, n0 * P:n1 * P].bitcast(FP8X4), scales=oscale[:, dg, n0 * P:n1 * P],
+                                      in_=rounded[n0, dg][:].rearrange("p n s -> p (n s)"))
 
-        def store_f32(n0, n1, dg):
-            rows = out_0[dg * K_PASS:(dg + 1) * K_PASS, n0 * P:n1 * P].rearrange("(p s) n -> p s n", s=PACK)
-            c0 = (n0 % 2) * P
-            nc.sync.dma_start(out=rows, in_=of32[n0 // 2, dg][:, :, c0:c0 + (n1 - n0) * P])
+        def store_result(n0, n1):
+            for dg in range(GROUPS):
+                rows = out_0[dg * K_PASS:(dg + 1) * K_PASS, n0 * P:n1 * P].rearrange("(p s) n -> p s n", s=PACK)
+                nc.sync.dma_start(out=rows, in_=result[n0 // 2, dg][:, :, result_cols(n0, n1)])
 
-        def store_words(n0, n1):
+        def store_codes(n0, n1):
             dst = out_1.rearrange("g p m t -> p g (m t)")[:, :, n0 * P * PACK:n1 * P * PACK]
             nc.sync.dma_start(out=dst.bitcast(I32), in_=ocode[:, :, n0 * P:n1 * P].bitcast(I32))
 
-        def store_scales():
-            for q in range(4):
-                dst = out_2[:, 4 * q:4 * q + 4, :].rearrange("g r n -> r g n")
-                nc.scalar.dma_start(out=dst.bitcast(I32), in_=oscale[32 * q:32 * q + 4, :, :].bitcast(I32))
+        def store_scales(n0, n1, queue):
+            for i in range(4):
+                dst = out_2[:, i:16:4, n0 * P:n1 * P].rearrange("g q n -> q g n")
+                queue.dma_start(out=dst.bitcast(I32), in_=oscale[i:P:32, :, n0 * P:n1 * P].bitcast(I32))
 
         batches = [
-            [(n, 0) for n in range(4)],
-            [(n, 1) for n in range(4)],
-            [(n, tg) for n in (4, 5) for tg in range(2)],
-            [(n, tg) for n in (6, 7) for tg in range(2)],
+            [(n, 0) for n in range(SPLIT_TILES)],
+            [(n, 1) for n in range(SPLIT_TILES)],
+            [(n, tg) for n in (4, 5) for tg in range(GROUPS)],
+            [(n, tg) for n in (6, 7) for tg in range(GROUPS)],
         ]
+        on_scalar, on_vector = nc.scalar.copy, nc.vector.tensor_copy
 
-        def each(fn, k, lo=0, hi=4):
-            for b in batches[k][lo:hi]:
-                fn(*b)
+        def each(step, banks, *more):
+            for n, tg in banks:
+                step(n, tg, *more)
 
-        def both(fn, n):
-            fn(n, 0)
-            fn(n, 1)
+        def both(step, *args):
+            for half in range(GROUPS):
+                step(*args, half)
 
-        def logs_and_rates(k):
-            for b in batches[k]:
-                log(*b)
-                rate(*b)
+        def logs_and_rates(banks):
+            for n, tg in banks:
+                log(n, tg)
+                rate(n, tg)
 
-        def turns(name, tg, jp, warm):
-            turn(name, tg, jp, 0, warm)
-            turn(name, tg, jp, 1, warm)
-
-        def quants(name, tg):
-            quant_act(name, tg, 0)
-            quant_act(name, tg, 1)
-
-        def casts(n0, n1, engine):
-            out_cast(n0, n1, 0, engine)
-            out_cast(n0, n1, 1, engine)
-
-        def out_quants(n0, n1):
-            out_quant(n0, n1, 0)
-            out_quant(n0, n1, 1)
-
-        def to_time(n):
+        def bcm_and_turn(n):
             bcm(n)
             both(turn_back, n)
 
@@ -357,124 +340,126 @@ def tile_bcmslidingthresholdtraceupdate_x2_kernel(
             quant_pm(n)
             both(correlate, n)
 
-        def stores(n0, n1):
-            store_f32(n0, n1, 0)
-            store_f32(n0, n1, 1)
+        def round_both(n0, n1, copy):
+            for dg in range(GROUPS):
+                round_result(n0, n1, dg, copy)
 
-        sort_words("r", 0, 0)
-        turns("r", 0, 0, "s")
-        sort_words("r", 0, 1)
-        late_loads()
-        turns("r", 0, 1, "s")
-        sort_words("x", 0, 0)
-        turns("x", 0, 0, "s")
+        sort_pairs("r", 0, 0)
+        both(turn, "r", 0, 0)
+        sort_pairs("r", 0, 1)
+        remaining_loads()
+        both(turn, "r", 0, 1)
+        sort_pairs("x", 0, 0)
+        both(turn, "x", 0, 0)
         quant_act("r", 0, 0)
-        sort_words("x", 0, 1)
+        sort_pairs("x", 0, 1)
         quant_act("r", 0, 1)
-        turns("x", 0, 1, "s")
-        for b in batches[0]:
-            drive(*b, 0, 2)
-        quants("x", 0)
-        for b in batches[0]:
-            drive(*b, 2, 4)
-            sigmoid(*b)
+        both(turn, "x", 0, 1)
+        each(drive, batches[0], 0, 2)
+        both(quant_act, "x", 0)
+        for n, tg in batches[0]:
+            drive(n, tg, 2, 4)
+            sigmoid(n, tg)
         both(trace_interleave, 0)
         trace_quant(0)
-        turns("x", 1, 0, "n")
-        turns("x", 1, 1, "n")
-        each(log, 0)
-        turns("r", 1, 0, "s")
-        turns("r", 1, 1, "s")
-        each(rate, 0, 0, 1)
-        quants("x", 1)
-        each(rate, 0, 1, 4)
-        for b in batches[1]:
-            drive(*b, 0, 2)
-        quants("r", 1)
-        for b in batches[1]:
-            drive(*b, 2, 4)
-        each(sigmoid, 1)
-        slope_half(0, 0)
-        slope_half(1, 0)
+
+        both(turn, "x", 1, 0)
+        both(turn, "x", 1, 1)
+        each(log, batches[0])
+        both(turn, "r", 1, 0)
+        both(turn, "r", 1, 1)
+        each(rate, batches[0][:1])
+        both(quant_act, "x", 1)
+        each(rate, batches[0][1:])
+        each(drive, batches[1], 0, 2)
+        both(quant_act, "r", 1)
+        each(drive, batches[1], 2, 4)
+        each(sigmoid, batches[1])
+        slope_of_pair(0, 0)
+        slope_of_pair(1, 0)
         both(trace_interleave, 1)
         nc.vector.tensor_scalar(out=neg_g[:], in0=g_raw[:], scalar1=-1.0, scalar2=None, op0=ALU.mult)
         trace_quant(1)
-        logs_and_rates(1)
-        each(drive, 2)
-        for n in range(4):
-            square(n)
-        each(sigmoid, 2)
-        slope_half(0, 1)
-        slope_half(1, 1)
-        to_time(0)
-        to_time(1)
+
+        logs_and_rates(batches[1])
+        each(drive, batches[2])
+        for n in range(SPLIT_TILES):
+            threshold(n)
+        each(sigmoid, batches[2])
+        slope_of_pair(0, 1)
+        slope_of_pair(1, 1)
+        bcm_and_turn(0)
+        bcm_and_turn(1)
         both(gain, 0)
         bcm(2)
         stage2(0)
         both(gain, 1)
         bcm(3)
         stage2(1)
-        logs_and_rates(2)
-        both(out_copy, 0)
-        both(out_copy, 1)
-        stores(0, 2)
-        each(drive, 3, 0, 2)
+
+        logs_and_rates(batches[2])
+        both(copy_result, 0)
+        both(copy_result, 1)
+        store_result(0, 2)
+        each(drive, batches[3][:2])
         both(turn_back, 2)
         both(turn_back, 3)
-        each(drive, 3, 2, 4)
-        square(4)
-        square(5)
-        each(sigmoid, 3)
+        each(drive, batches[3][2:])
+        threshold(4)
+        threshold(5)
+        each(sigmoid, batches[3])
         slope(4)
         slope(5)
         both(gain, 2)
-        out_cast(0, 2, 0, "v")
+        round_result(0, 2, 0, on_vector)
         stage2(2)
         both(gain, 3)
         bcm(4)
         stage2(3)
-        both(out_copy, 2)
+        both(copy_result, 2)
         both(turn_back, 4)
         bcm(5)
-        out_cast(0, 2, 1, "v")
+        round_result(0, 2, 1, on_vector)
         both(gain, 4)
-        out_quants(0, 2)
-        store_words(0, 2)
+        quant_result(0, 2)
+        store_codes(0, 2)
         stage2(4)
-        logs_and_rates(3)
-        both(out_copy, 3)
-        stores(2, 4)
+
+        logs_and_rates(batches[3])
+        both(copy_result, 3)
+        store_result(2, 4)
         both(turn_back, 5)
-        square(6)
-        square(7)
+        threshold(6)
+        threshold(7)
         slope(6)
         both(gain, 5)
-        both(out_copy, 4)
-        stores(4, 5)
-        casts(2, 4, "s")
-        to_time(6)
+        both(copy_result, 4)
+        store_result(4, 5)
+        round_both(2, 4, on_scalar)
+        bcm_and_turn(6)
         stage2(5)
         slope(7)
-        both(out_copy, 5)
-        stores(5, 6)
+        both(copy_result, 5)
+        store_result(5, 6)
         both(gain, 6)
-        to_time(7)
+        bcm_and_turn(7)
         stage2(6)
-        out_quants(2, 4)
-        store_words(2, 4)
-        both(out_copy, 6)
-        stores(6, 7)
+        quant_result(2, 4)
+        store_codes(2, 4)
+        store_scales(0, 4, nc.sync)
+        both(copy_result, 6)
+        store_result(6, 7)
         both(gain, 7)
-        out_cast(4, 6, 0, "v")
+        round_result(4, 6, 0, on_vector)
         stage2(7)
-        out_cast(4, 6, 1, "v")
-        casts(6, 7, "s")
-        out_quants(4, 6)
-        store_words(4, 6)
-        out_quants(6, 7)
-        both(out_copy, 7)
-        stores(7, 8)
-        casts(7, 8, "v")
-        out_quants(7, 8)
-        store_words(6, 8)
-        store_scales()
+        round_result(4, 6, 1, on_vector)
+        round_both(6, 7, on_scalar)
+        quant_result(4, 6)
+        store_codes(4, 6)
+        quant_result(6, 7)
+        both(copy_result, 7)
+        store_result(7, 8)
+        round_both(7, 8, on_vector)
+        quant_result(7, 8)
+        store_codes(6, 8)
+        store_scales(4, 8, nc.scalar)

from contextlib import ExitStack

import concourse.mybir as mybir
from concourse.masks import make_identity

T, D, R, N = 1024, 1024, 1024, 1024
FLOPS = 2 * T * D * N + 2 * T * R * N + 2 * D * T * N

F32 = mybir.dt.float32
BF16 = mybir.dt.bfloat16
U32 = mybir.dt.uint32
I32 = mybir.dt.int32
U8 = mybir.dt.uint8
FP8X4 = mybir.dt.float8_e4m3fn_x4
FP4X4 = mybir.dt.float4_e2m1fn_x4
ALU = mybir.AluOpType
ACT = mybir.ActivationFunctionType

P = 128
PACK = 4
K_PASS = P * PACK
GROUPS = 2
N_TILES = N // P
BANK = 512
DRIVE_BANKS = 4
SPLIT_TILES = 4
LATE_TILES = 6
LINEAR_FROM = 20.0
INV_SQRT_T = 1.0 / 32.0


def tile_bcmslidingthresholdtraceupdate_x2_kernel(
    tc, x, w_words, w_scales, r, l_words, l_scales, trace, g, out_0, out_1, out_2
):
    nc = tc.nc
    with ExitStack() as ctx:
        keep = ctx.enter_context(tc.tile_pool(name="keep", bufs=1))
        work = ctx.enter_context(tc.tile_pool(name="work", bufs=1))
        psum = ctx.enter_context(tc.psum_pool(name="psum", bufs=1))
        ctx.enter_context(tc.manual_schedule())

        ident = keep.tile([P, P], F32, name="ident")
        make_identity(nc, ident[:])

        wscale = {}
        for uh in range(2):
            for name in ("l", "w"):
                wscale[name, uh] = keep.tile([P, GROUPS, BANK], U8, name="scale_%s%d" % (name, uh), align_bytes=64)
                nc.vector.memset(wscale[name, uh][:].rearrange("p g n -> p (g n)").bitcast(I32), 0)

        act_src = {"x": x, "r": r}
        words_src = {"w": w_words, "l": l_words}
        scales_src = {"w": w_scales, "l": l_scales}
        raw = {}
        wcode = {}
        traw = {}

        def load_act(name, tg, jp):
            raw[name, tg, jp] = work.tile([P, 2, D], BF16, name="raw", tag="raw", bufs=6, align_bytes=64)
            rows = act_src[name][tg * K_PASS:(tg + 1) * K_PASS, :].rearrange("(p j) k -> p j k", j=PACK)
            nc.sync.dma_start(out=raw[name, tg, jp][:], in_=rows[:, 2 * jp:2 * jp + 2, :])

        def load_words(name, uh):
            wcode[name, uh] = keep.tile([P, GROUPS, N], U8, name="words_%s%d" % (name, uh), align_bytes=64)
            src = words_src[name][:, :, uh * N:(uh + 1) * N].rearrange("g p b -> p g b")
            nc.sync.dma_start(out=wcode[name, uh][:].bitcast(I32), in_=src.bitcast(I32))

        def load_scales(name, uh):
            for i in range(4):
                src = scales_src[name][:, i:16:4, uh * BANK:(uh + 1) * BANK].rearrange("g q n -> q g n")
                nc.sync.dma_start(out=wscale[name, uh][i:P:32, :, :].bitcast(I32), in_=src.bitcast(I32))

        def load_trace(tg):
            traw[tg] = keep.tile([P, PACK, D], BF16, name="traw%d" % tg, align_bytes=64)
            rows = trace[tg * K_PASS:(tg + 1) * K_PASS, :].rearrange("(p j) d -> p j d", j=PACK)
            nc.sync.dma_start(out=traw[tg][:], in_=rows)

        load_act("r", 0, 0)
        load_act("r", 0, 1)
        load_scales("l", 0)
        load_words("l", 0)
        load_act("x", 0, 0)
        load_act("x", 0, 1)
        load_scales("w", 0)
        load_words("w", 0)
        load_trace(0)
        load_act("x", 1, 0)
        load_act("x", 1, 1)
        g_raw = keep.tile([P, GROUPS, PACK], BF16, name="g_raw")

        def remaining_loads():
            load_act("r", 1, 0)
            load_act("r", 1, 1)
            load_trace(1)
            load_words("l", 1)
            load_words("w", 1)
            load_scales("l", 1)
            load_scales("w", 1)
            nc.sync.dma_start(out=g_raw[:], in_=g.rearrange("(g p j) -> p g j", g=GROUPS, j=PACK))

        sorted_pairs = {}
        grouped = {}
        acode = {}
        ascale = {}

        def sort_pairs(name, tg, jp):
            sorted_pairs[name, tg, jp] = work.tile([P, 4, 2, P], F32, name="sorted_pairs", tag="sorted_pairs", bufs=2)
            dst = sorted_pairs[name, tg, jp]
            rows = raw[name, tg, jp][:].rearrange("p j k -> p (j k)")
            if name == "r":
                nc.vector.tensor_copy(out=dst[:], in_=rows.bitcast(F32).rearrange("p (c q u) -> p c u q", c=4, u=2))
            else:
                src = rows.rearrange("p (c q u e) -> p c u q e", c=4, u=2, e=2)
                for u in range(2):
                    nc.vector.tensor_scalar(
                        out=dst[:, :, u, :].bitcast(BF16).rearrange("p c (q e) -> p c q e", e=2),
                        in0=src[:, :, u, :, :], scalar1=-1.0, scalar2=None, op0=ALU.mult)

        def turn(name, tg, jp, kp):
            bank = psum.tile([P, 2, 2, P], F32, name="tbank", tag="bank%d" % (DRIVE_BANKS + 2 * jp + kp))
            pairs = raw[name, tg, jp][:].rearrange("p j k -> p (j k)").bitcast(F32)
            for jj in range(2):
                for u in range(2):
                    if tg == 0:
                        src = sorted_pairs[name, tg, jp][:, 2 * jj + kp, u, :]
                    else:
                        base = jj * (D // 2) + kp * 2 * P
                        src = pairs[:, base + u:base + 2 * P:2]
                    nc.tensor.transpose(bank[:, u, jj, :], src, ident[:])
            if jp == 0:
                grouped[name, tg, kp] = work.tile([P, PACK * BANK], BF16, name="grouped", tag="grouped", bufs=4,
                                                  align_bytes=64)
            dst = grouped[name, tg, kp][:, jp * 2 * BANK:(jp + 1) * 2 * BANK]
            if name == "x" and tg == 1:
                src = bank[:].rearrange("p u j t -> p (u j t)").bitcast(BF16).rearrange("p (u c e) -> p c u e", u=2, e=2)
                nc.vector.tensor_scalar(out=dst.rearrange("p (c u e) -> p c u e", u=2, e=2), in0=src,
                                        scalar1=-1.0, scalar2=None, op0=ALU.mult)
            else:
                nc.scalar.copy(out=dst.bitcast(F32).rearrange("p (c u) -> p c u", u=2),
                               in_=bank[:].rearrange("p u j t -> p (j t) u"))

        def quant_act(name, tg, kp):
            acode[name, tg, kp] = keep.tile([P, BANK], U32, name="acode_%s%d%d" % (name, tg, kp), align_bytes=64)
            ascale[name, tg, kp] = keep.tile([P, BANK], U8, name="ascale_%s%d%d" % (name, tg, kp), align_bytes=64)
            nc.vector.quantize_mx(out=acode[name, tg, kp][:].bitcast(FP8X4), scales=ascale[name, tg, kp][:],
                                  in_=grouped[name, tg, kp][:])

        tgrouped = {}
        tcode = {}
        tscale = {}

        def trace_interleave(tg, dg):
            if dg == 0:
                tgrouped[tg] = work.tile([P, GROUPS, PACK * BANK], BF16, name="tgrouped", tag="tgrouped", bufs=1,
                                         align_bytes=64)
            nc.vector.tensor_copy(
                out=tgrouped[tg][:, dg, :].rearrange("p (s m j) -> p s m j", s=PACK, j=PACK),
                in_=traw[tg][:, :, dg * K_PASS:(dg + 1) * K_PASS].rearrange("p j (m s) -> p s m j", s=PACK))

        def trace_quant(tg):
            tcode[tg] = keep.tile([P, D], U32, name="tcode%d" % tg, align_bytes=64)
            tscale[tg] = keep.tile([P, D], U8, name="tscale%d" % tg, align_bytes=64)
            nc.vector.quantize_mx(out=tcode[tg][:].bitcast(FP8X4), scales=tscale[tg][:],
                                  in_=tgrouped[tg][:].rearrange("p h c -> p (h c)"))

        zbank = {}
        q_two = {}
        q_one = {}
        log_q = {}
        neg_a = {}
        slope_a = {}
        neg_phi = {}
        theta = keep.tile([P, N_TILES], F32, name="theta")
        neg_g = keep.tile([P, GROUPS, PACK], F32, name="neg_g")

        product_order = {0: (("r", "l"), ("x", "w")), 1: (("x", "w"), ("r", "l"))}

        def drive(n, tg, first=0, last=4):
            if first == 0:
                bank = n if n < SPLIT_TILES else 2 * (n % 2) + tg
                zbank[n, tg] = psum.tile([P, BANK], F32, name="zbank", tag="bank%d" % bank)
            uh, col = divmod(n, N_TILES // 2)
            passes = [(a_name, w_name, kp) for a_name, w_name in product_order[tg] for kp in range(GROUPS)]
            for i in range(first, last):
                a_name, w_name, kp = passes[i]
                nc.tensor.matmul_mx(
                    out=zbank[n, tg][:],
                    lhsT=wcode[w_name, uh][:, kp, col * 2 * P:(col + 1) * 2 * P].bitcast(FP4X4),
                    lhsT_scale=wscale[w_name, uh][:, kp, col * P:(col + 1) * P],
                    rhs=acode[a_name, tg, kp][:].bitcast(FP8X4),
                    rhs_scale=ascale[a_name, tg, kp][:],
                    start=(i == 0), stop=(i == len(passes) - 1))

        def sigmoid(n, tg):
            key, row = ((n // 2, tg), n % 2) if n < SPLIT_TILES else (n, tg)
            if row == 0:
                q_two[key] = work.tile([P, 2, BANK], F32, name="q_two", tag="q_two", bufs=4)
            q_one[n, tg] = q_two[key][:, row, :]
            nc.scalar.activation(out=q_one[n, tg], in_=zbank[n, tg][:], func=ACT.Sigmoid)

        def log(n, tg):
            log_q[n, tg] = work.tile([P, BANK], F32, name="log_q", tag="log_q", bufs=4)
            nc.scalar.activation(out=log_q[n, tg][:], in_=q_one[n, tg], func=ACT.Ln)

        def rate(n, tg):
            if tg == 0 and n % 2 == 0:
                neg_a[n // 2] = work.tile([P, 2, GROUPS, BANK], F32, name="neg_a", tag="neg_a", bufs=3)
            nc.vector.scalar_tensor_tensor(out=neg_a[n // 2][:, n % 2, tg, :], in0=log_q[n, tg][:], scalar=-LINEAR_FROM,
                                           in1=zbank[n, tg][:], op0=ALU.max, op1=ALU.min)

        def all_time(of_pairs, n):
            return of_pairs[n // 2][:, n % 2, :, :].rearrange("p g t -> p (g t)")

        def threshold(n):
            squares = work.tile([P, T], BF16, name="squares", tag="squares", bufs=1)
            nc.scalar.activation(out=squares[:], in_=all_time(neg_a, n), func=ACT.Square,
                                 scale=INV_SQRT_T, accum_out=theta[:, n:n + 1])

        def slope_of_pair(pair, tg):
            if tg == 0:
                slope_a[pair] = work.tile([P, 2, GROUPS, BANK], F32, name="slope_a", tag="slope_a", bufs=3)
            nc.vector.scalar_tensor_tensor(out=slope_a[pair][:, :, tg, :], in0=q_two[pair, tg][:], scalar=1.0,
                                           in1=neg_a[pair][:, :, tg, :], op0=ALU.subtract, op1=ALU.mult)

        def slope(n):
            if n % 2 == 0:
                slope_a[n // 2] = work.tile([P, 2, GROUPS, BANK], F32, name="slope_a", tag="slope_a", bufs=3)
            nc.vector.scalar_tensor_tensor(out=all_time(slope_a, n), in0=q_two[n][:].rearrange("p g t -> p (g t)"),
                                           scalar=1.0, in1=all_time(neg_a, n), op0=ALU.subtract, op1=ALU.mult)

        def bcm(n):
            neg_phi[n] = work.tile([P, T], F32, name="neg_phi", tag="neg_phi", bufs=2)
            nc.vector.scalar_tensor_tensor(out=neg_phi[n][:], in0=all_time(neg_a, n), scalar=theta[:, n:n + 1],
                                           in1=all_time(slope_a, n), op0=ALU.add, op1=ALU.mult)

        def banks_of(n):
            return 2 * (n % 2) + (DRIVE_BANKS if n < LATE_TILES else 0)

        pbank = {}
        pm = {}
        pcode = {}
        pscale = {}

        def turn_back(n, tg):
            pbank[n, tg] = psum.tile([P, PACK, P], F32, name="pbank", tag="bank%d" % (banks_of(n) + tg))
            for j in range(PACK):
                nc.tensor.transpose(pbank[n, tg][:, j, :], neg_phi[n][:, tg * BANK + j * P:tg * BANK + (j + 1) * P],
                                    ident[:])

        def gain(n, tg):
            if tg == 0:
                pm[n] = work.tile([P, GROUPS, P, PACK], BF16, name="pm", tag="pm", bufs=2, align_bytes=64)
            nc.vector.tensor_tensor(out=pm[n][:, tg, :, :], in0=pbank[n, tg][:].rearrange("p j n -> p n j"),
                                    in1=neg_g[:, tg, :].unsqueeze(1).to_broadcast([P, P, PACK]), op=ALU.mult)

        def quant_pm(n):
            pcode[n] = work.tile([P, GROUPS * P], U32, name="pcode", tag="pcode", bufs=2, align_bytes=64)
            pscale[n] = work.tile([P, GROUPS * P], U8, name="pscale", tag="pscale", bufs=2, align_bytes=64)
            nc.vector.quantize_mx(out=pcode[n][:].bitcast(FP8X4), scales=pscale[n][:],
                                  in_=pm[n][:].rearrange("p g n j -> p (g n j)"))

        obank = {}
        result = {}
        rounded = {}
        ocode = keep.tile([P, GROUPS, N], U32, name="ocode", align_bytes=64)
        oscale = keep.tile([P, GROUPS, N], U8, name="oscale", align_bytes=64)

        def correlate(n, dg):
            obank[n, dg] = psum.tile([P, PACK, P], F32, name="obank", tag="bank%d" % (banks_of(n) + dg))
            for s in range(PACK):
                cols = slice(dg * BANK + s * P, dg * BANK + (s + 1) * P)
                for tg in range(GROUPS):
                    nc.tensor.matmul_mx(
                        out=obank[n, dg][:, s, :],
                        lhsT=tcode[tg][:, cols].bitcast(FP8X4),
                        lhsT_scale=tscale[tg][:, cols],
                        rhs=pcode[n][:, tg * P:(tg + 1) * P].bitcast(FP8X4),
                        rhs_scale=pscale[n][:, tg * P:(tg + 1) * P],
                        start=(tg == 0), stop=(tg == GROUPS - 1))

        def result_cols(n0, n1):
            return slice((n0 % 2) * P, (n0 % 2 + n1 - n0) * P)

        def copy_result(n, dg):
            if n % 2 == 0:
                result[n // 2, dg] = work.tile([P, PACK, 2 * P], F32, name="result", tag="result", bufs=4)
            nc.scalar.activation(out=result[n // 2, dg][:, :, result_cols(n, n + 1)], in_=obank[n, dg][:],
                                 func=ACT.Copy, scale=INV_SQRT_T)

        def round_result(n0, n1, dg, copy):
            rounded[n0, dg] = work.tile([P, (n1 - n0) * P, PACK], BF16, name="rounded", tag="rounded", bufs=4,
                                        align_bytes=64)
            copy(out=rounded[n0, dg][:], in_=result[n0 // 2, dg][:, :, result_cols(n0, n1)].rearrange("p s n -> p n s"))

        def quant_result(n0, n1):
            for dg in range(GROUPS):
                nc.vector.quantize_mx(out=ocode[:, dg, n0 * P:n1 * P].bitcast(FP8X4), scales=oscale[:, dg, n0 * P:n1 * P],
                                      in_=rounded[n0, dg][:].rearrange("p n s -> p (n s)"))

        def store_result(n0, n1):
            for dg in range(GROUPS):
                rows = out_0[dg * K_PASS:(dg + 1) * K_PASS, n0 * P:n1 * P].rearrange("(p s) n -> p s n", s=PACK)
                nc.sync.dma_start(out=rows, in_=result[n0 // 2, dg][:, :, result_cols(n0, n1)])

        def store_codes(n0, n1):
            dst = out_1.rearrange("g p m t -> p g (m t)")[:, :, n0 * P * PACK:n1 * P * PACK]
            nc.sync.dma_start(out=dst.bitcast(I32), in_=ocode[:, :, n0 * P:n1 * P].bitcast(I32))

        def store_scales(n0, n1, queue):
            for i in range(4):
                dst = out_2[:, i:16:4, n0 * P:n1 * P].rearrange("g q n -> q g n")
                queue.dma_start(out=dst.bitcast(I32), in_=oscale[i:P:32, :, n0 * P:n1 * P].bitcast(I32))

        batches = [
            [(n, 0) for n in range(SPLIT_TILES)],
            [(n, 1) for n in range(SPLIT_TILES)],
            [(n, tg) for n in (4, 5) for tg in range(GROUPS)],
            [(n, tg) for n in (6, 7) for tg in range(GROUPS)],
        ]
        on_scalar, on_vector = nc.scalar.copy, nc.vector.tensor_copy

        def each(step, banks, *more):
            for n, tg in banks:
                step(n, tg, *more)

        def both(step, *args):
            for half in range(GROUPS):
                step(*args, half)

        def logs_and_rates(banks):
            for n, tg in banks:
                log(n, tg)
                rate(n, tg)

        def bcm_and_turn(n):
            bcm(n)
            both(turn_back, n)

        def stage2(n):
            quant_pm(n)
            both(correlate, n)

        def round_both(n0, n1, copy):
            for dg in range(GROUPS):
                round_result(n0, n1, dg, copy)

        sort_pairs("r", 0, 0)
        both(turn, "r", 0, 0)
        sort_pairs("r", 0, 1)
        remaining_loads()
        both(turn, "r", 0, 1)
        sort_pairs("x", 0, 0)
        both(turn, "x", 0, 0)
        quant_act("r", 0, 0)
        sort_pairs("x", 0, 1)
        quant_act("r", 0, 1)
        both(turn, "x", 0, 1)
        each(drive, batches[0], 0, 2)
        both(quant_act, "x", 0)
        for n, tg in batches[0]:
            drive(n, tg, 2, 4)
            sigmoid(n, tg)
        both(trace_interleave, 0)
        trace_quant(0)

        both(turn, "x", 1, 0)
        both(turn, "x", 1, 1)
        each(log, batches[0])
        both(turn, "r", 1, 0)
        both(turn, "r", 1, 1)
        each(rate, batches[0][:1])
        both(quant_act, "x", 1)
        each(rate, batches[0][1:])
        each(drive, batches[1], 0, 2)
        both(quant_act, "r", 1)
        each(drive, batches[1], 2, 4)
        each(sigmoid, batches[1])
        slope_of_pair(0, 0)
        slope_of_pair(1, 0)
        both(trace_interleave, 1)
        nc.vector.tensor_scalar(out=neg_g[:], in0=g_raw[:], scalar1=-1.0, scalar2=None, op0=ALU.mult)
        trace_quant(1)

        logs_and_rates(batches[1])
        each(drive, batches[2])
        for n in range(SPLIT_TILES):
            threshold(n)
        each(sigmoid, batches[2])
        slope_of_pair(0, 1)
        slope_of_pair(1, 1)
        bcm_and_turn(0)
        bcm_and_turn(1)
        both(gain, 0)
        bcm(2)
        stage2(0)
        both(gain, 1)
        bcm(3)
        stage2(1)

        logs_and_rates(batches[2])
        both(copy_result, 0)
        both(copy_result, 1)
        store_result(0, 2)
        each(drive, batches[3][:2])
        both(turn_back, 2)
        both(turn_back, 3)
        each(drive, batches[3][2:])
        threshold(4)
        threshold(5)
        each(sigmoid, batches[3])
        slope(4)
        slope(5)
        both(gain, 2)
        round_result(0, 2, 0, on_vector)
        stage2(2)
        both(gain, 3)
        bcm(4)
        stage2(3)
        both(copy_result, 2)
        both(turn_back, 4)
        bcm(5)
        round_result(0, 2, 1, on_vector)
        both(gain, 4)
        quant_result(0, 2)
        store_codes(0, 2)
        stage2(4)

        logs_and_rates(batches[3])
        both(copy_result, 3)
        store_result(2, 4)
        both(turn_back, 5)
        threshold(6)
        threshold(7)
        slope(6)
        both(gain, 5)
        both(copy_result, 4)
        store_result(4, 5)
        round_both(2, 4, on_scalar)
        bcm_and_turn(6)
        stage2(5)
        slope(7)
        both(copy_result, 5)
        store_result(5, 6)
        both(gain, 6)
        bcm_and_turn(7)
        stage2(6)
        quant_result(2, 4)
        store_codes(2, 4)
        store_scales(0, 4, nc.sync)
        both(copy_result, 6)
        store_result(6, 7)
        both(gain, 7)
        round_result(4, 6, 0, on_vector)
        stage2(7)
        round_result(4, 6, 1, on_vector)
        round_both(6, 7, on_scalar)
        quant_result(4, 6)
        store_codes(4, 6)
        quant_result(6, 7)
        both(copy_result, 7)
        store_result(7, 8)
        round_both(7, 8, on_vector)
        quant_result(7, 8)
        store_codes(6, 8)
        store_scales(4, 8, nc.scalar)
